import numpy as np, ml_dtypes
CORES = [23,119,17,113]
N = 4
import mx_ref
BF = ml_dtypes.bfloat16
def gentries(a):
    return np.ascontiguousarray(a.reshape(8, 16, -1).transpose(0, 2, 1)).reshape(8, -1)
def gtable(e):
    e = np.asarray(e); return np.ascontiguousarray(e.reshape(8, -1, 16).transpose(0, 2, 1)).reshape(128, -1).astype(np.int32)
def gcols(t, e):
    v = np.concatenate([t.reshape(8, 16, -1, 4), np.zeros((8, 16, 1, 4), BF)], axis=2)
    return np.ascontiguousarray(np.stack([v[g][:, e[g]] for g in range(8)])).reshape(128, -1)
def tile(rs):
    return np.stack(rs, axis=2).reshape(128, -1).astype(BF)
def cut(t, i, w=512):
    return t[:, w * i:w * i + w]
def pick(q, e):
    c = np.concatenate([q[0].reshape(128, -1, 4), np.zeros((128, 1, 4), np.uint8)], axis=1); s = np.concatenate([q[1], np.ones((16, 1), np.uint8)], axis=1)
    return (np.ascontiguousarray(c[:, e].reshape(128, -1)), np.ascontiguousarray(s[:, e]))
def join(*qs):
    return (np.concatenate([q[0] for q in qs], axis=1), np.concatenate([q[1] for q in qs], axis=1))
def put(q, e, v):
    c, s = q[0].reshape(128, -1, 4).copy(), q[1].copy(); c[:, e] = v[0].reshape(128, -1, 4); s[:, e] = v[1]
    return (c.reshape(128, -1), s)
def pk(c, s):
    return (np.ascontiguousarray(c), mx_ref.live(s))
def emit(q):
    return q[0], q[1]
def packed(v, rng):
    q = [mx_ref.quantize(np.ascontiguousarray(v[r])) for r in range(N)]
    return np.stack([a for a, b in q]), np.stack([mx_ref.plane(b, rng) for a, b in q])
def values_of_codes():
    e, c = np.zeros((128, 128, 4), np.float32), np.zeros((128, 2, 4), np.uint8)
    e[np.arange(128), np.arange(128), 0] = 1
    c[:127, :, 0] = np.arange(256).reshape(2, 128).T[:127]
    return mx_ref.matmul(mx_ref.quantize(e.reshape(128, 512).astype(BF)), (c.reshape(128, 8), np.full((16, 2), 127, np.uint8))).T.reshape(-1).astype(np.float64)
CODE_VALUE, SCALE_VALUE = values_of_codes(), 2.0 ** (np.arange(256) - 127.0)
def decode(q):
    return (CODE_VALUE[q[0]].reshape(16, 8, -1, 4) * SCALE_VALUE[q[1]][:, None, :, None] + 0.0).reshape(128, -1).astype(np.float32)
def f(rng, *shape):
    return mx_ref.flush((rng.standard_normal(shape, dtype=np.float32) * np.exp2(rng.integers(-2, 3, shape[:-1] + (1,)))).astype(BF))
def wide(rng, *shape, cols=0):
    v = rng.standard_normal(shape, dtype=np.float32) * np.exp2(rng.integers(-12, 13, shape)).astype(np.float32)
    if cols: v *= np.repeat(np.exp2(rng.integers(-cols, cols + 1, shape[:-2] + (1, shape[-1] // 4))) * (rng.random(shape[:-2] + (1, shape[-1] // 4)) > 0.0625), 4, axis=-1).astype(np.float32)
    return mx_ref.flush(v.astype(BF))
C, B, R = 512, 32, 3
STEP = [1, 2, 3]
def slides(s):
    n = 8 * B
    i = np.arange(n)
    who = np.full((n, 5, 5), -9)
    key = np.full((n, 5, 5), -np.inf, np.float32)
    who[:, :4, :4] = np.arange(16).reshape(4, 4)
    key[:, :4, :4] = s.reshape(n, 4, 4)
    left = np.zeros((4, n), np.int64)
    for k in range(4):
        left[k] = who[:, 0, 0]
        y, c = np.zeros(n, np.int64), np.zeros(n, np.int64)
        for m in range(6):
            right = key[i, y, c + 1] >= key[i, y + 1, c]
            y2, c2 = np.where(right, y, y + 1), np.where(right, c + 1, c)
            go = who[i, y2, c2] >= 0
            j = i[go]
            who[j, y[go], c[go]] = who[j, y2[go], c2[go]]
            key[j, y[go], c[go]] = key[j, y2[go], c2[go]]
            y, c = np.where(go, y2, y), np.where(go, c2, c)
        who[i, y, c] = -1 - k
        key[i, y, c] = -np.inf
    b = np.arange(B)
    w = who[:, :4, :4].reshape(8, B, 16)
    stand = np.where(w >= 0, 16 * b[:, None] + w, C + B * (-1 - w) + b[:, None]).reshape(8, C)
    return (left.reshape(4, 8, B) + 16 * b).transpose(1, 0, 2).reshape(8, 4 * B), stand
def big(v):
    v = v.astype(np.float32)
    v[np.abs(v) < np.float32(2.0 ** -16)] = 0
    return v.astype(BF)
def seats(rng):
    return np.argsort(rng.random((N, 8, C)), axis=2)
def seated(e, a):
    s = np.zeros_like(a)
    np.put_along_axis(s, e, a, axis=2)
    return s
def digits(s):
    return ((s[..., None] >> np.arange(4)) & 1) * np.exp2(np.arange(4.0))
def numbers_of(rng, e):
    return {"x": big(f(rng, N, 128, 4 * C)), "p": np.stack([gtable(e[r]) for r in range(N)]), "u": np.array(f(rng, N, 128, 512)), "v": np.array(f(rng, N, 128, 512))}
def layers(rng, still=()):
    w = big(f(rng, N, 128, 2048)).reshape(N, 8, 16, 4, 8, 16, 4)
    for i in still:
        w[:, :, i] = 0
        w[:, :, :, :, :, i] = 0
    return w.reshape(N, 128, 2048)
def weights(rng, w):
    c, s = packed(np.ascontiguousarray(w).reshape(N, 128, 2048), rng)
    return {"wc": c, "ws": s}
def signs(rng):
    return np.stack([rng.permutation(8) % 2 * 2.0 - 1.0 for r in range(N)])
def setup_inputs(rng):
    return {**numbers_of(rng, seats(rng)), **weights(rng, layers(rng))}
def setup_inputs_ties(rng):
    d = numbers_of(rng, seats(rng))
    e = rng.permutation(N)
    x = d["x"].reshape(N, 8, 16, C, 4)
    for r in range(N):
        k = np.zeros(C, int) if r == e[0] else rng.permutation(C) % 3
        a = x[r][:, :8, :3].copy()
        a[:, :, 2] = 0
        x[r][:, :8] = a[:, :, k]
    x[e[1]] = 0
    u = d["u"].reshape(N, 8, 16, 8, 16, 4)
    k = u.copy()
    u[:, :, :, :, 0] = 0
    for g in range(8): u[:, g, :8, g, 0] = k[:, g, :8, g, 0]
    return {"x": x.reshape(N, 128, 4 * C), "p": d["p"], "u": u.reshape(N, 128, 512), "v": d["v"], **weights(rng, layers(rng, range(8)))}
def setup_inputs_near(rng):
    e = seats(rng)
    d = numbers_of(rng, e)
    x = d["x"].astype(np.float32).reshape(N, 8, 16, C, 4)
    u = d["u"].reshape(N, 128, 128, 4)
    u[:, :, ::16] = 0
    o, c = rng.permutation(N) % 4, signs(rng)
    s = seated(e, np.argsort(rng.random((N, 8, B, 16)), axis=3).reshape(N, 8, C))
    x[:, :, 0] = 0
    x[:, :, 9] = 0
    for r in range(N):
        size = 2.0 ** -23 if o[r] < 2 else 2.0 ** -30
        if o[r] < 2:
            x[r, :, 0, :, 0] = c[r][:, None]
            x[r, :, 9, :, 0] = c[r][:, None] * 2.0 ** -12
            for i in rng.permutation(8)[:4]: x[r, i, 0, rng.integers(C), 0] *= np.float32(2.0 ** 30)
        x[r, :, 8] = digits(s[r]) * (-size if o[r] == 3 else size) + 0.0
        x[r, :, 10:] = rng.integers(4, 8, (8, 6, C, 4)) * rng.choice([-1.0, 1.0], (8, 6, C, 4)) * size
        k = 1.0 if o[r] == 0 else 2.0 ** -30
        for h in range(0, 128, 16):
            u[r, h, h, 0] = k
            u[r, h + 8, h] = k
            u[r, h + 9, h, 0] = k
    return {"x": x.reshape(N, 128, 4 * C).astype(BF), "p": d["p"], "u": u.reshape(N, 128, 512), "v": d["v"], **weights(rng, layers(rng, [0, 8, 9, 10, 11, 12, 13, 14, 15]))}
def setup_inputs_huge(rng):
    d = numbers_of(rng, seats(rng))
    c = np.stack([rng.permutation(C) % 2 * 2.0 - 1.0 for r in range(N)])
    c[rng.permutation(N) < N // 2] = -1
    x = 2.0 ** 30 * (1 - 0.0625 * (rng.random((N, 128, C, 4)) < 0.25)) * c[:, None, :, None]
    u = d["u"].reshape(N, 128, 128, 4)
    a = 2.0 ** 30 * (1 - 0.0625 * (rng.random((N, 128, 8, 4)) < 0.25)) * signs(rng)[:, None, :, None]
    u[:, :, ::16] = a.astype(np.float32).astype(BF)
    w = np.zeros((N, 128, 4, 128, 4), np.float32)
    i = np.arange(128)
    for b in range(4): w[:, i, b, i, b] = -32
    return {"x": x.astype(np.float32).reshape(N, 128, 4 * C).astype(BF), "p": d["p"], "u": u.reshape(N, 128, 512), "v": d["v"], **weights(rng, w.astype(BF))}
def setup_inputs_moves(rng):
    e = seats(rng)
    i = rng.permutation(N)
    e[i[2]] = np.arange(C)
    d = numbers_of(rng, e)
    a = np.arange(16)
    s = np.argsort(rng.random((N, 8, B, 16)), axis=3)
    k = np.argsort(rng.random((N, 8, B)), axis=2) % 4
    k[i[0]], k[i[1]] = 0, 1
    s[k == 0] = a % 4 * 4 + a // 4
    s[k == 1] = a
    x = d["x"].reshape(N, 8, 16, C, 4)
    x[:, :, 8] = digits(seated(e, s.reshape(N, 8, C))).astype(np.float32).astype(BF)
    u = d["u"].reshape(N, 128, 128, 4)
    u[:, :, ::16] = 0
    for h in range(0, 128, 16): u[:, h + 8, h] = 1
    return {"x": x.reshape(N, 128, 4 * C), "p": d["p"], "u": u.reshape(N, 128, 512), "v": d["v"], **weights(rng, layers(rng, range(8, 16)))}
def setup_inputs_spread(rng):
    d = setup_inputs(rng)
    d["x"] = big(wide(rng, N, 128, 4 * C, cols=6))
    return d
def check_inputs(d):
    b = []
    for k in ("x", "u", "v"):
        a = np.abs(d[k].astype(np.float32))
        if not (np.isfinite(a).all() and ((a == 0) | (a >= 2.0 ** -30) & (a <= 2.0 ** 30)).all()): b.append("a value of " + k)
    none, least, most = [emit(mx_ref.quantize(np.full((128, 16), k, np.float32).astype(BF)))[1][0, 0] for k in (0.0, 2.0 ** -30, 2.0 ** 30)]
    for r in range(N):
        if not (np.sort(gentries(d["p"][r]), axis=1) == np.arange(C)).all(): b.append("p: a group's entries aren't all columns, each once")
        if ((d["wc"][r] == 0x7F) | (d["wc"][r] == 0xFF)).any(): b.append("wc: a code that is no number")
        s = mx_ref.live(d["ws"][r])
        if ((s != none) & ((s < least) | (s > most))).any(): b.append("ws: a scale out of range")
    return b
def reference(x, p, u, v, wc, ws):
    qu = [mx_ref.quantize(u[r]) for r in range(N)]
    lay = [pk(wc[r], ws[r]) for r in range(N)]
    seat = [gentries(p[r]) for r in range(N)]
    slots = np.tile(C + np.arange(4 * B), (8, 1))
    now = [x[r] for r in range(N)]
    for t in range(R):
        sent, fill = [], []
        for r in range(N):
            s = mx_ref.matmul(qu[r], mx_ref.quantize(now[r]))
            left, stand = slides(np.take_along_axis(s[::16], seat[r], axis=1))
            sent.append(mx_ref.quantize(gcols(now[r], np.take_along_axis(seat[r], left, axis=1))))
            fill.append(np.take_along_axis(np.concatenate([seat[r], slots], axis=1), stand, axis=1))
        came = decode(join(*sent)).astype(BF)
        made = []
        for r in range(N):
            z = gcols(np.concatenate([now[r], cut(came, (r - STEP[t]) % N, 16 * B)], axis=1), fill[r])
            q = mx_ref.quantize(z)
            made.append(tile([np.maximum(mx_ref.matmul(pick(lay[r], np.arange(128 * b, 128 * b + 128)), q), np.float32(0.0)) * np.float32(0.015625) + z[:, b::4].astype(np.float32) for b in range(4)]))
        now = made
    y, ol = np.zeros((N, 128, C), np.float32), np.zeros((N, 8, C), np.float32)
    oc, osc = np.zeros((N, 128, 4 * C), np.uint8), np.zeros((N, 16, C), np.uint8)
    for r in range(N):
        q = mx_ref.quantize(now[r])
        y[r] = mx_ref.matmul(mx_ref.quantize(v[r]), q)
        ol[r] = fill[r]
        oc[r], osc[r] = emit(q)
    return {"y": y, "ol": ol, "oc": oc, "osc": osc}

@@ -1,0 +1,456 @@
+from concourse.mybir import dt, AluOpType as A, ActivationFunctionType as AF
+
+F32, BF, I32, U16, U8, X4 = "float32", "bfloat16", "int32", "uint16", "uint8", "float8_e4m3fn_x4"
+STEP = [1, 2, 3]
+SENT = -1.0e29
+JS = 152
+ORDER = ("L_0 Gb0 Ga0 Gb1 C0 QV0 Ga1 QV1 R_0 C1 L_1 X0 R_1 A_0 A_1 QT0 FD Gb2 Gc2 Gb3 QV2 SC0 QT1 SH0 R_2 Ga3 X1 SC1 QV3 R_3 X2 "
+         "A_2 A_3 QT2 QT3 SC2 SH1 SC3")
+
+SCRATCH = {"ps": ("psum", [128, 4096], F32), "ptp": ("sbuf", [128, 5, 10], F32), "k0": ("sbuf", [128, 5, 11], F32)}
+for _ty, _bufs in (
+        (BF, dict(us=512, vs=512, ones=520, zt=520, dd=2048, tc0=2560, tc1=2560, tc2=2560, tc3=2560)),
+        (X4, dict(qu=128, qv=128, qw=512, qe=512, qn=512, qz=512, qt0=512, qt1=512, qt2=512, qt3=512, lc0=512, lc1=512, lc2=512)),
+        (U8, dict(su=128, sv=128, sw=512, se=512, sn=512, sz=512, st0=512, st1=512, st2=512, st3=512, ls0=512, ls1=512, ls2=512)),
+        (I32, dict(pi=68, w1=66, w2=66, w3=66, w4=66, w5=66, ip=4, cb=4, iq=32, sm=40)),
+        (U16, dict(lst=16, oa=32, ob=32, posl=32, off=128, oln=32, ll0=32, ll1=32, ll2=32, sl0=32, sl1=32, sl2=32)),
+        (F32, dict(pf=64, pt=64, pf2=66, pt2=64, col=12, jb=6 * JS, d0=120, dk=120, ko=150, non=40, gg=50, yy=120, cd=120, cc=120,
+                   lf=32, lft=32, in2=128, in2t=128, ln=32, lnt=32, ssb=512, kr=512, tp=512, a32=2048, olt=640, olr=512, ysb=512))):
+    for _k, _n in _bufs.items():
+        SCRATCH[_k] = ("sbuf", [128, _n], _ty)
+
+SEMAPHORES = ["cv", "cs", "cp", "cg", "x0", "x1", "x2", "x3", "lu", "lp", "lw", "lv", "snd", "outs", "wa0", "wa1", "wa2", "wa3"] + \
+    ["ar%d_%d" % (t, h) for t in range(3) for h in range(2)] + ["al%d" % t for t in range(3)]
+
+
+def rank_program(g, core, T, topo):
+    rank = T.rank_of(core)
+    if rank is None:
+        return
+    N = len(T.cores)
+    Q = {"v": g.vector, "s": g.scalar, "p": g.tensor, "g": g, "y": g.sync}
+    CSEM = {"v": "cv", "s": "cs", "p": "cp", "g": "cg"}
+    count = {"cv": 0, "cs": 0, "cp": 0, "cg": 0, "snd": 0, "outs": 0, "wa0": 0, "wa1": 0, "wa2": 0, "wa3": 0}
+    waited = {q: {} for q in Q}
+    writer, readers = {}, {}
+
+    def need(q, reads, writes):
+        ev = {}
+        for k in list(reads) + list(writes):
+            if k in writer:
+                s, n = writer[k]
+                ev[s] = max(ev.get(s, 0), n)
+        for k in writes:
+            for s, n in readers.get(k, {}).items():
+                ev[s] = max(ev.get(s, 0), n)
+        for s in sorted(ev):
+            if waited[q].get(s, 0) < ev[s]:
+                Q[q].wait_ge(T.sem[s], ev[s])
+                waited[q][s] = ev[s]
+
+    def note(ev, reads, writes):
+        for k in reads:
+            d = readers.setdefault(k, {})
+            d[ev[0]] = max(d.get(ev[0], 0), ev[1])
+        for k in writes:
+            writer[k] = ev
+            readers[k] = {}
+
+    def op(q, fn, reads, writes):
+        need(q, reads, writes)
+        s = CSEM[q]
+        fn().then_inc(T.sem[s], 1)
+        count[s] += 1
+        note((s, count[s]), reads, writes)
+
+    def load(q, sem, total, out, in_, writes):
+        Q[q].dma_start(out, in_).then_inc(T.sem[sem], 16)
+        note((sem, total), [], writes)
+
+    def store(q, out, in_, reads):
+        need(q, reads, [])
+        Q[q].dma_start(out, in_).then_inc(T.sem.outs, 16)
+        count["outs"] += 16
+
+    V = g.vector
+
+    def tt(o, a, b, o_, r, w):
+        op("v", lambda: V.tensor_tensor(o, a, b, o_), r, w)
+
+    def ts(o, a, s1, s2, o0, o1, r, w):
+        if o1 is None:
+            op("v", lambda: V.tensor_scalar(o, a, s1, None, o0), r, w)
+        else:
+            op("v", lambda: V.tensor_scalar(o, a, s1, s2, o0, o1), r, w)
+
+    def cp(o, a, r, w):
+        op("v", lambda: V.tensor_copy(o, a), r, w)
+
+    def tr(o, a, r, w):
+        op("v", lambda: V.transpose(o, a), r, w)
+
+    def ms(o, c, w):
+        op("v", lambda: V.memset(o, c), [], w)
+
+    def scan(o, a, b, init, o0, o1, r, w):
+        op("v", lambda: V.tensor_tensor_scan(o, a, b, init, o0, o1), r, w)
+
+    def quant(q, s, a, r, w):
+        op("v", lambda: V.quantize_mx(q, s, a), r, w)
+
+    def act(o, a, r, w, func=AF.Copy, **kw):
+        op("s", lambda: g.scalar.activation(o, a, func, **kw), r, w)
+
+    def iota(o, pat, base, cm, w, flt=False):
+        if flt:
+            op("g", lambda: g.iota(o, pat, base, cm, allow_small_or_imprecise_dtypes=True), [], w)
+        else:
+            op("g", lambda: g.iota(o, pat, base, cm), [], w)
+
+    bank = [0]
+
+    def mm(n, lq, lsc, rq, rsc, r):
+        b = bank[0] % 8
+        bank[0] += 1
+        op("p", lambda: g.tensor.matmul_mx(T.ps[:, 512 * b:512 * b + n], lq, lsc, rq, rsc, True, True), r, ["ps%d" % b])
+        return b
+
+    def send(t, out, in_, sem, reads):
+        dst = T.cores[(rank + STEP[t]) % N]
+        rid, pid = topo.addr(dst)[0:2]
+        need("g", reads, [])
+        g.remote_dma(out, in_, T.sem[sem], T.sem.snd, pid, rid, topo.mask(core, dst))
+        count["snd"] += len(topo.engines(core, dst))
+
+    def arriving(t):
+        return len(topo.engines(T.cores[(rank - STEP[t]) % N], core))
+
+    for t in range(3):
+        for h in range(2):
+            writer["land%d_%d" % (t, h)] = ("ar%d_%d" % (t, h), 2 * arriving(t))
+        writer["ll%d" % t] = ("al%d" % t, arriving(t))
+    writer["land0_0"] = writer["land0_1"] = ("ar0_0", 3 * arriving(0))
+
+    def send_codes(t, m0, m1, sem):
+        send(t, T["lc%d" % t][:, 128 * m0:128 * m1].bitcast(dt.uint8), T["qt%d" % t][:, 128 * m0:128 * m1].bitcast(dt.uint8), sem,
+             ["qt%d_%d" % (t, m) for m in range(m0, m1)])
+
+    def send_scales(t, m0, m1, sem):
+        send(t, T["ls%d" % t][:, 128 * m0:128 * m1], T["st%d" % t][:, 128 * m0:128 * m1], sem, ["qt%d_%d" % (t, m) for m in range(m0, m1)])
+
+    def send_half(t, h):
+        send_codes(t, 2 * h, 2 * h + 2, "ar%d_%d" % (t, h))
+        send_scales(t, 2 * h, 2 * h + 2, "ar%d_%d" % (t, h))
+
+    def pk(t, m):
+        return ["tc%d_%d_0" % (t, m), "tc%d_%d_1" % (t, m)]
+
+    for m in range(4):
+        load("y", "x%d" % m, 16, T.tc0[:, 512 * m:512 * m + 512], T.x[:, 512 * m:512 * m + 512], pk(0, m))
+    load("s", "lu", 16, T.us[:], T.u[:], ["us"])
+    load("s", "lp", 144, T.pi[:, 0:32], T.p[:], ["pi"])
+    for a in range(4):
+        for h in range(2):
+            load("s", "lp", 144, T.pi[32 * a:32 * a + 32, 32 + 16 * h:48 + 16 * h], T.p[32 * a + 16 * h:32 * a + 16 * h + 16, :], ["pi"])
+    load("s", "lw", 32, T.qw[:].bitcast(dt.uint8), T.wc[:], ["w"])
+    load("s", "lw", 32, T.sw[:], T.ws[:], ["w"])
+    load("s", "lv", 16, T.vs[:], T.v[:], ["vs"])
+
+    iota(T.ip[:], [[0, 4]], 0, 1, ["ip"])
+    iota(T.cb[:], [[4, 4]], 0, 0, ["cb"])
+    ms(T.ones[:], 1.0, ["ones"])
+    op("g", lambda: g.affine_select(T.zt[:], T.ones[:], [[-1, 520]], A.is_equal, 0.0, 3, 4), ["ones"], ["zt"])
+    iota(T.iq[:], [[4, 32]], 0, 0, ["iq"])
+    ms(T.k0[:], SENT, ["k0"])
+    ms(T.ko[:], SENT, ["ko"])
+    ms(T.d0[:], 0.0, ["right", "on"])
+    ms(T.dk[:], 0.0, ["wn", "pk"])
+    ms(T.gg[:], 1.0, ["g0", "g1", "g2", "gc"])
+    ms(T.cd[:], -1.0e9, ["cd"])
+    ms(T.gg[:, 0:4], 0.0, ["gc"])
+    ms(T.gg[:, 5:9], 0.0, ["gc2"])
+    ms(T.cd[:, 0:120:3], 1.0e9, ["cd"])
+    sm, col = T.sm, T.col
+    ts(sm[:, 16:20], T.ip[:], 31, None, A.bitwise_and, None, ["ip"], ["sj"])
+    ts(sm[:, 0:4], T.ip[:], 2, 3, A.arith_shift_right, A.bitwise_and, ["ip"], ["sr"])
+    ts(sm[:, 20:21], T.ip[:, 0:1], 3, None, A.bitwise_and, None, ["ip"], ["st"])
+    ts(col[:, 1:2], sm[:, 16:17], 16.0, 2060.0, A.mult, A.add, ["sj"], ["m3"])
+    ts(col[:, 4:8], sm[:, 16:20], 48.0, 6168.0, A.mult, A.add, ["sj"], ["yb0"])
+    tt(sm[:, 4:8], sm[:, 0:4], T.cb[:], A.add, ["sr", "cb"], ["sm"])
+    cp(col[:, 0:1], sm[:, 20:21], ["st"], ["tcol"])
+    act(T.jb[:, 0:3 * JS], T.ones[:, 0:3 * JS], ["ones", "m3"], ["j0", "j1", "j2", "tu0", "tu1", "tu2"], AF.Identity, bias=col[:, 1:2], scale=0.0)
+    act(T.ptp[:], T.ones[:, 0:50], ["ones", "m3"], ["ptp0", "ptp1"], AF.Identity, bias=col[:, 1:2], scale=0.0)
+    act(T.jb[:, 3 * JS:6 * JS], T.ones[:, 0:3 * JS], ["ones", "m3"], ["j3", "j4", "j5", "tu3", "tu4", "tu5"], AF.Identity, bias=col[:, 1:2], scale=0.0)
+    ts(sm[:, 21:22], sm[:, 0:1], 10.0, None, A.mult, None, ["sr"], ["s10"])
+    ts(sm[:, 24:25], sm[:, 0:1], 1.0, None, A.min, None, ["sr"], ["smin"])
+    ts(sm[:, 8:12], sm[:, 4:8], 43.0, None, A.mult, None, ["sm"], ["si"])
+    tt(col[:, 8:12], col[:, 4:8], T.cb[:], A.add, ["yb0", "cb"], ["yb"])
+    tt(sm[:, 22:23], sm[:, 0:1], sm[:, 24:25], A.add, ["sr", "smin"], ["ska"])
+    ts(sm[:, 28:32], sm[:, 8:12], 7, None, A.arith_shift_right, None, ["si"], ["si2"])
+    tt(sm[:, 23:24], sm[:, 21:22], sm[:, 20:21], A.add, ["s10", "st"], ["snat"])
+    ts(sm[:, 15:16], sm[:, 21:22], 3.0, None, A.add, None, ["s10"], ["sx3"])
+    ts(sm[:, 32:36], sm[:, 28:32], 7.0, None, A.mult, None, ["si2"], ["si3"])
+    for h in range(2):
+        ts(T.lst[:, 8 + h:9 + h], sm[:, 22:23], float(JS), 2.0 + 15 * h, A.mult, A.add, ["ska"], ["lfa%d" % h])
+        ts(T.lst[:, 10 + h:11 + h], sm[:, 0:1], float(JS), JS + 2.0 + 15 * h, A.mult, A.add, ["sr"], ["lfb%d" % h])
+        ts(T.lst[:, 12 + h:13 + h], sm[:, 23:24], 3.0, 2.0 + 15 * h, A.mult, A.add, ["snat"], ["lnl%d" % h])
+    tt(sm[:, 12:15], sm[:, 4:7], sm[:, 32:35], A.add, ["sm", "si3"], ["sx"])
+    ts(T.pi[:, 64:66], T.ip[:, 0:2], 15, None, A.bitwise_and, None, ["ip"], ["pi2"])
+    for h in range(2):
+        ts(T.lst[:, h:8:2], sm[:, 12:16], 3.0, 2.0 + 15 * h, A.mult, A.add, ["sx", "sx3"], ["la%d" % h])
+
+    def tu(s):
+        o = s * JS
+        tt(T.jb[:, o:o + 117:3], T.jb[:, o + 5:o + 122:3], T.jb[:, o + 32:o + 149:3], A.subtract, ["j%d" % s], ["t%d" % s, "tu%d" % s])
+
+    def uu(s):
+        o = s * JS
+        tt(T.jb[:, o + 1:o + 118:3], T.jb[:, o + 32:o + 149:3], T.jb[:, o + 2:o + 119:3], A.subtract, ["j%d" % s], ["u%d" % s])
+
+    def first_ids(s, pt, key):
+        return [lambda: ts(T.ptp[:, 0:4, 0:4], pt[:, 0:16], 4.0, None, A.mult, None, [key], ["ptp0"]),
+                lambda: ts(T.ptp[:, 0:4, 5:9], pt[:, 16:32], 4.0, None, A.mult, None, [key], ["ptp1"]),
+                lambda: cp(T.jb[:, s * JS + 2:s * JS + 150:3], T.ptp[:], ["ptp0", "ptp1"], ["j%d" % s]),
+                lambda: tu(s), lambda: uu(s)]
+
+    pi = T.pi[:, 0:66]
+    later = [
+        lambda: ts(T.w1[:], pi, 3, None, A.bitwise_and, None, ["pi", "pi2"], ["w1"]),
+        lambda: ts(T.w2[:], pi, 2, 3, A.arith_shift_right, A.bitwise_and, ["pi", "pi2"], ["w2"]),
+        lambda: ts(T.w3[:], pi, 2, 124, A.arith_shift_right, A.bitwise_and, ["pi", "pi2"], ["w3"]),
+        lambda: ts(T.w4[:], T.w1[:], 3.0, None, A.is_equal, None, ["w1"], ["w4"]),
+        lambda: ts(T.w5[:], T.w2[:], -2.0, 9.0, A.mult, A.add, ["w2"], ["w5"]),
+        lambda: ts(T.w2[:], T.w2[:], 3.0, None, A.mult, None, ["w2"], ["w2"]),
+        lambda: tt(T.w4[:], T.w4[:], T.w5[:], A.mult, ["w4", "w5"], ["w4"]),
+        lambda: tt(T.w1[:], T.w1[:], T.w2[:], A.add, ["w1", "w2"], ["w1"]),
+        lambda: tt(T.w1[:], T.w1[:], T.w4[:], A.add, ["w1", "w4"], ["w1"]),
+        lambda: ts(T.w2[:], T.w1[:], 2, None, A.arith_shift_right, None, ["w1"], ["w2"]),
+        lambda: tt(T.w3[:], T.w3[:], T.w1[:], A.add, ["w1", "w3"], ["w3"]),
+        lambda: ts(T.w2[:], T.w2[:], 124.0, None, A.mult, None, ["w2"], ["w2"]),
+        lambda: tt(T.pf2[:], T.w3[:], T.w2[:], A.add, ["w2", "w3"], ["pf2"]),
+        lambda: tr(T.pt2[:], T.pf2[:, 0:64], ["pf2"], ["pt2"]),
+        lambda: ts(T.posl[:], T.iq[:], T.pf2[:, 64:65], None, A.add, None, ["pf2", "iq"], ["posl"]),
+        lambda: cp(T.ob[:], T.pt2[:, 32:64], ["pt2"], ["ob"]),
+    ] + first_ids(1, T.pt2, "pt2")
+
+    def some(n):
+        for _ in range(n):
+            if later:
+                later.pop(0)()
+
+    def key_piece(t, m):
+        return mm(128, T.qu[:], T.su[:], T["qt%d" % t][:, 128 * m:128 * m + 128], T["st%d" % t][:, 128 * m:128 * m + 128], ["qu", "qt%d_%d" % (t, m)])
+
+    def key_copy(m, b):
+        act(T.ssb[:, 128 * m:128 * m + 128], T.ps[:, 512 * b:512 * b + 128], ["ps%d" % b], ["ssb%d" % m])
+
+    def qt_piece(t, m):
+        quant(T["qt%d" % t][:, 128 * m:128 * m + 128], T["st%d" % t][:, 128 * m:128 * m + 128], T["tc%d" % t][:, 512 * m:512 * m + 512],
+              pk(t, m), ["qt%d_%d" % (t, m)])
+
+    for b in range(4):
+        quant(T.qe[:, 128 * b:128 * b + 128], T.se[:, 128 * b:128 * b + 128], T.zt[:, 3 - b:515 - b], ["zt"], ["e%d" % b])
+    quant(T.qu[:], T.su[:], T.us[:], ["us"], ["qu"])
+    ids0 = first_ids(0, T.pt, "pt")
+    for m in range(4):
+        qt_piece(0, m)
+        key_copy(m, key_piece(0, m))
+        if m == 0:
+            send_codes(0, 0, 1, "ar0_0")
+        if m == 1:
+            cp(T.pf[:], T.pi[:, 0:64], ["pi"], ["pf"])
+        if m == 2:
+            tr(T.pt[:], T.pf[:], ["pf"], ["pt"])
+        if m == 3:
+            send_codes(0, 1, 4, "ar0_0")
+            send_scales(0, 0, 4, "ar0_0")
+            cp(T.oa[:], T.pt[:, 32:64], ["pt"], ["oa"])
+            ids0[0]()
+            ids0[1]()
+    later[0:0] = ids0[2:]
+
+    ssb_keys = ["ssb%d" % m for m in range(4)]
+
+    for t in range(3):
+        tc, nx = T["tc%d" % t], T["tc%d" % (t + 1)]
+        tck = [k for m in range(4) for k in pk(t, m)]
+        ok, okk = (T.oa, "oa") if t == 0 else (T.ob, "ob")
+        some(1)
+        cp(T.kr[:, 0:128], T.ssb[:].indirect(ok[:, 0:8]), ssb_keys + [okk], ["kr0"])
+        for i in range(1, 4):
+            act(T.kr[:, 128 * i:128 * i + 128], T.ssb[:].indirect(ok[:, 8 * i:8 * i + 8]), ssb_keys + [okk], ["kr%d" % i])
+        for i in range(4):
+            if i != 1:
+                some(1)
+            tr(T.tp[:, 128 * i:128 * i + 128], T.kr[:, 128 * i:128 * i + 128], ["kr%d" % i], ["tp%d" % i])
+        some(1)
+        for h in range(2):
+            cp(T.k0[:, 0:4, 5 * h:5 * h + 4], T.tp[:, 16 * h:512:32], ["tp0", "tp1", "tp2", "tp3"], ["k0_%d" % h] + (["k0"] if h == 0 else []))
+        some(1)
+
+        def unpack(h):
+            for b in range(4):
+                bk = mm(256, T.qe[:, 128 * b:128 * b + 128], T.se[:, 128 * b:128 * b + 128], T["lc%d" % t][:, 256 * h:256 * h + 256],
+                        T["ls%d" % t][:, 256 * h:256 * h + 256], ["e%d" % b, "land%d_%d" % (t, h)])
+                act(T.dd[:, 1024 * h + b:1024 * h + 1024:4], T.ps[:, 512 * bk:512 * bk + 256], ["ps%d" % bk], ["dd%d_%d" % (h, b)])
+
+        def mark(k):
+            o = (k + 2) * JS
+            act(T.yy[:, k:117:3], T.jb[:, o + 2:o + 119:3], ["j%d" % (k + 2), "t%d" % (k + 2), "u%d" % (k + 2), "yb"], ["yy%d" % k], AF.Identity,
+                bias=col[:, 8 + k:9 + k], scale=-2.0)
+
+        unpack(0)
+        for k in range(4):
+            s = (0 if t == 0 else 1) if k == 0 else k + 1
+            so = k + 2
+            if k == 0:
+                kc, kr_, kd, n, kk = T.k0[:, 0:4, 0:10], T.k0[:, 0:4, 1:11], T.k0[:, 1:5, 0:10], 40, ["k0", "k0_0", "k0_1"]
+            else:
+                kc, kr_, kd, n, kk = T.ko[:, 2:119:3], T.ko[:, 5:122:3], T.ko[:, 32:149:3], 39, ["ko"]
+            jin = ["right", "on", "j%d" % s, "t%d" % s, "u%d" % s]
+            jout = ["j%d" % so, "t%d" % so, "u%d" % so, "tu%d" % so]
+            tt(T.d0[:, 1:3 * n:3], kr_, kd, A.is_ge, kk, ["right"])
+            if k < 3:
+                tt(T.dk[:, 1:3 * n:3], kr_, kd, A.max, kk, ["wn"])
+            else:
+                uu(s)
+            for i in range(3):
+                scan(T.gg[:, 10 * i + 10:10 * i + 20], T.d0[:, 30 * i + 1:30 * i + 30:3], T.gg[:, 10 * i:10 * i + 10], 1.0, A.mult, A.max,
+                     ["right", "gc", "gc2"] + (["g%d" % (i - 1)] if i else []), ["g%d" % i])
+                if 0 < k < 3 and i == 0:
+                    uu(s)
+                elif k == 2 and i == 1:
+                    scan(T.jb[:, so * JS:so * JS + 18], T.d0[:, 0:18], T.jb[:, s * JS:s * JS + 18], 0.0, A.mult, A.add, jin, jout)
+                elif k == 2:
+                    c0 = 8 if t == 0 else 10
+                    slabs = [x % z for x in ("j%d", "t%d", "u%d") for z in range(5)]
+                    cp(T.lf[:], T.jb[:, 0:5 * JS].indirect(T.lst[:, c0:c0 + 2]), slabs + ["lfa0", "lfa1", "lfb0", "lfb1"], ["lf"])
+                else:
+                    some(1)
+            if k > 0:
+                if k == 2:
+                    unpack(1)
+                mark(k - 1)
+            gk = ["g0", "g1", "g2"]
+            if k < 3:
+                tt(T.non[:, 0:n], T.gg[:, 9:9 + n], T.gg[:, 0:n], A.is_le, gk, ["non"])
+            if k == 2:
+                tr(T.lft[:], T.lf[:], ["lf"], ["lft"])
+            tt(T.d0[:, 2:117:3], T.gg[:, 9:48], T.gg[:, 0:39], A.is_gt, gk, ["on"])
+            if k == 2:
+                ts(T["sl%d" % t][:], T.lft[:], col[:, 0:1], None, A.add, None, ["lft", "tcol"], ["sl%d" % t])
+                send(t, T["ll%d" % t][:], T["sl%d" % t][:], "al%d" % t, ["sl%d" % t])
+            if k < 3:
+                tt(T.dk[:, 2:3 * n:3], T.non[:, 0:n], kc, A.mult, kk + ["non"], ["pk"])
+            scan(T.jb[:, so * JS:so * JS + 117], T.d0[:, 0:117], T.jb[:, s * JS:s * JS + 117], 0.0, A.mult, A.add, jin, jout)
+            if k < 3:
+                scan(T.ko[:, 0:117], T.d0[:, 0:117], T.dk[:, 0:117], 0.0, A.mult, A.add, ["right", "on", "wn", "pk"], ["ko"])
+                tu(so)
+
+        win = T.jb[:, 5 * JS:6 * JS]
+
+        def lists(hf):
+            cp(T.in2[:, 64 * hf:64 * hf + 64], win.indirect(T.lst[:, 4 * hf:4 * hf + 4]), ["j5", "t5", "u5", "la0", "la1"], ["in2_%d" % hf])
+            tr(T.in2t[:, 64 * hf:64 * hf + 64], T.in2[:, 64 * hf:64 * hf + 64], ["in2_%d" % hf], ["in2t%d" % hf])
+            ts(T.off[:, 64 * hf:64 * hf + 64], T.in2t[:, 64 * hf:64 * hf + 64], col[:, 0:1], None, A.add, None, ["in2t%d" % hf, "tcol"], ["off%d" % hf])
+
+        def gather(q, m, c0, c1):
+            w = tc[:, 0:2048] if m < 2 else tc[:, 0:2560]
+            r = tck + ["off%d" % (m // 2)] + ([] if m < 2 else ["fd%d" % t])
+            o = nx[:, 512 * m + 16 * c0:512 * m + 16 * c1]
+            (cp if q == "v" else act)(o, w.indirect(T.off[:, 32 * m + c0:32 * m + c1]), r, pk(t + 1, m)[c0 // 16:c1 // 16])
+
+        def qv(m):
+            quant(T.qz[:, 128 * m:128 * m + 128], T.sz[:, 128 * m:128 * m + 128], nx[:, 512 * m:512 * m + 512], pk(t + 1, m), ["qz%d" % m])
+            return [mm(128, T.qw[:, 128 * b:128 * b + 128], T.sw[:, 128 * b:128 * b + 128], T.qz[:, 128 * m:128 * m + 128],
+                       T.sz[:, 128 * m:128 * m + 128], ["w", "qz%d" % m]) for b in range(4)]
+
+        def relu(m, banks):
+            for b in range(4):
+                act(T.a32[:, 512 * m + b:512 * m + 512:4], T.ps[:, 512 * banks[b]:512 * banks[b] + 128], ["ps%d" % banks[b]], ["a%d_%d" % (m, b)],
+                    AF.Relu, scale=0.015625)
+
+        bk, sk = {}, {}
+
+        def step(name):
+            k, m = name[0:2], int(name[2:] or 0)
+            ak = ["a%d_%d" % (m, b) for b in range(4)]
+            piece = nx[:, 512 * m:512 * m + 512]
+            if k == "L_":
+                lists(m)
+            elif k[0] == "G":
+                q, c0, c1 = {"Ga": ("v", 0, 16), "Gb": ("s", 16, 32), "Gc": ("s", 0, 16), "Gd": ("v", 16, 32), "Gs": ("s", 0, 32), "Gv": ("v", 0, 32)}[k]
+                gather(q, m, c0, c1)
+            elif k == "QV":
+                bk[m] = qv(m)
+            elif k == "R_":
+                relu(m, bk[m])
+            elif k == "A_":
+                tt(piece, T.a32[:, 512 * m:512 * m + 512], piece, A.add, ak + pk(t + 1, m), pk(t + 1, m))
+            elif k == "D_":
+                need("g", ak, pk(t + 1, m))
+                g.dma_start(piece, T.a32[:, 512 * m:512 * m + 512], accum_op=A.add).then_inc(T.sem["wa%d" % m], 16)
+                count["wa%d" % m] += 16
+                note(("wa%d" % m, count["wa%d" % m]), ak, pk(t + 1, m))
+            elif k == "QT":
+                qt_piece(t + 1, m)
+                if t < 2:
+                    sk[m] = key_piece(t + 1, m)
+            elif k == "SC":
+                if t < 2:
+                    key_copy(m, sk[m])
+            elif k == "SH":
+                if t < 2:
+                    send_half(t + 1, m)
+            elif k == "C0":
+                scan(T.cc[:, 0:117], T.cd[:, 0:117], T.yy[:, 0:117], 0.0, A.max, A.min, ["cd", "yy0", "yy1", "yy2"], ["cc"])
+            elif k == "C1":
+                tt(T.jb[:, 5 * JS + 2:5 * JS + 119:3], T.jb[:, 5 * JS + 2:5 * JS + 119:3], T.cc[:, 2:117:3], A.min, ["j5", "cc"], ["j5"])
+            elif k in ("FD", "FV"):
+                (act if k == "FD" else cp)(tc[:, 2048:2560], T.dd[:].indirect(T["ll%d" % t][:]),
+                                           ["dd%d_%d" % (h, b) for h in range(2) for b in range(4)] + ["ll%d" % t], ["fd%d" % t])
+            elif k == "X0":
+                if t == 0:
+                    iota(T.olt[:, 0:128], [[16, 32], [1, 4]], 0, 0, ["olt0"], True)
+                    iota(T.olt[:, 256:384], [[16, 32], [1, 4]], 11, 0, ["olt2"], True)
+                    iota(T.olt[:, 128:256], [[16, 32], [3, 2], [1, 2]], 5, 0, ["olt1"], True)
+                    iota(T.olt[:, 3:128:4], [[16, 32]], 4, 0, ["olt0"], True)
+                if t == 1:
+                    iota(T.olt[:, 256:384:4], [[16, 32]], 10, 0, ["olt2"], True)
+                    iota(T.olt[:, 384:512], [[16, 32], [4, 4]], 3, 0, ["olt3"], True)
+                    iota(T.olt[:, 512:640], [[1, 32], [32, 4]], 512, 0, ["olt4"], True)
+            elif k == "X1":
+                if t == 0:
+                    some(32)
+                if t == 1:
+                    quant(T.qv[:], T.sv[:], T.vs[:], ["vs"], ["qv"])
+                if t == 2:
+                    cp(T.ln[:], win.indirect(T.lst[:, 12:14]), ["j5", "t5", "u5", "lnl0", "lnl1"], ["ln"])
+                    tr(T.lnt[:], T.ln[:], ["ln"], ["lnt"])
+                    ts(T.oln[:], T.lnt[:], 0.25, None, A.mult, None, ["lnt"], ["oln"])
+            elif k == "X2":
+                if t == 2:
+                    act(T.olr[:], T.olt[:].indirect(T.oln[:]), ["oln"] + ["olt%d" % i for i in range(5)], ["olr"])
+                    store("y", T.ol[:], T.olr[0:128:16, :], ["olr"])
+
+        for name in ORDER.split():
+            step(name)
+
+    qk = ["qt3_%d" % m for m in range(4)] + ["posl"]
+    banks = []
+    for h in range(2):
+        lo, hi = 256 * h, 256 * h + 256
+        cp(T.qn[:, lo:hi].bitcast(dt.uint32), T.qt3[:, 0:512].bitcast(dt.uint32).indirect(T.posl[:, 16 * h:16 * h + 16]), qk, ["qn%d" % h])
+        act(T.sn[:, lo:hi], T.st3[:, 0:512].indirect(T.posl[:, 16 * h:16 * h + 16]), qk, ["sn%d" % h])
+        banks.append(mm(256, T.qv[:], T.sv[:], T.qn[:, lo:hi], T.sn[:, lo:hi], ["qv", "qn%d" % h, "sn%d" % h]))
+        store("y", T.oc[:, 4 * lo:4 * hi], T.qn[:, lo:hi].bitcast(dt.uint8), ["qn%d" % h])
+    act(T.ysb[:, 0:256], T.ps[:, 512 * banks[0]:512 * banks[0] + 256], ["ps%d" % banks[0]], ["y0"])
+    cp(T.ysb[:, 256:512], T.ps[:, 512 * banks[1]:512 * banks[1] + 256], ["ps%d" % banks[1]], ["y1"])
+    store("y", T.y[:, 0:256], T.ysb[:, 0:256], ["y0"])
+    store("y", T.y[:, 256:512], T.ysb[:, 256:512], ["y1"])
+    for k in range(4):
+        store("s", T.osc[4 * k:4 * k + 4, :], T.sn[32 * k:32 * k + 4, :], ["sn0", "sn1"])
+
+    for s in sorted(count):
+        if count[s]:
+            g.wait_ge(T.sem[s], count[s])

@@ -6,6 +6,7 @@ SENT = -1.0e29
 JS = 152
 ORDER = ("L_0 Gb0 Ga0 Gb1 C0 QV0 Ga1 QV1 R_0 C1 L_1 X0 R_1 A_0 A_1 QT0 FD Gb2 Gc2 Gb3 QV2 SC0 QT1 SH0 R_2 Ga3 X1 SC1 QV3 R_3 X2 "
          "A_2 A_3 QT2 QT3 SC2 SH1 SC3")
+WAKE, FAR, FARL, SLACK = 200, 4000, 2800, 40
 
 SCRATCH = {"ps": ("psum", [128, 4096], F32), "ptp": ("sbuf", [128, 5, 10], F32), "k0": ("sbuf", [128, 5, 11], F32)}
 for _ty, _bufs in (
@@ -14,13 +15,72 @@ for _ty, _bufs in (
         (U8, dict(su=128, sv=128, sw=512, se=512, sn=512, sz=512, st0=512, st1=512, st2=512, st3=512, ls0=512, ls1=512, ls2=512)),
         (I32, dict(pi=68, w1=66, w2=66, w3=66, w4=66, w5=66, ip=4, cb=4, iq=32, sm=40)),
         (U16, dict(lst=16, oa=32, ob=32, posl=32, off=128, oln=32, ll0=32, ll1=32, ll2=32, sl0=32, sl1=32, sl2=32)),
-        (F32, dict(pf=64, pt=64, pf2=66, pt2=64, col=12, jb=6 * JS, d0=120, dk=120, ko=150, non=40, gg=50, yy=120, cd=120, cc=120,
+        (F32, dict(pf=64, pt=64, pf2=66, pt2=64, col=12, jb=6 * JS, d0=120, dk=150, ko=150, non=40, gg=60, yy=120, cd=120, cc=120,
+                   e0=120, e1=120, rr=120, c01=40,
                    lf=32, lft=32, in2=128, in2t=128, ln=32, lnt=32, ssb=512, kr=512, tp=512, a32=2048, olt=640, olr=512, ysb=512))):
     for _k, _n in _bufs.items():
         SCRATCH[_k] = ("sbuf", [128, _n], _ty)
 
-SEMAPHORES = ["cv", "cs", "cp", "cg", "x0", "x1", "x2", "x3", "lu", "lp", "lw", "lv", "snd", "outs", "wa0", "wa1", "wa2", "wa3"] + \
+SEMAPHORES = ["cv", "cs", "cp", "cg", "x0", "x1", "x2", "x3", "lu", "lp", "lw", "lv", "snd", "outs"] + \
     ["ar%d_%d" % (t, h) for t in range(3) for h in range(2)] + ["al%d" % t for t in range(3)]
+
+
+def schedule(nodes, ready):
+    deps, wr, rd, far = [], {}, {}, {}
+    for i, nd in enumerate(nodes):
+        if nd[5]:
+            far.setdefault(nd[5][0], []).append((i, nd[5][1]))
+    for i, nd in enumerate(nodes):
+        d = {}
+        for k in list(nd[2]) + list(nd[3]):
+            if k in wr:
+                d[wr[k]] = WAKE
+            for j, lat in far.get(k, []):
+                d[j] = lat
+        for k in nd[3]:
+            for j in rd.get(k, []):
+                d[j] = WAKE
+        d.pop(i, None)
+        deps.append(d)
+        for k in nd[2]:
+            rd.setdefault(k, []).append(i)
+        for k in nd[3]:
+            wr[k] = i
+            rd[k] = []
+    n = len(nodes)
+    succ = [[] for _ in range(n)]
+    for i in range(n):
+        for j in deps[i]:
+            succ[j].append(i)
+    pri = [0.0] * n
+    for i in range(n - 1, -1, -1):
+        pri[i] = nodes[i][1] + max([deps[j][i] + pri[j] for j in succ[i]] + [0])
+    left = [len(d) for d in deps]
+    cand = [i for i in range(n) if not left[i]]
+    end, free, order = [0.0] * n, {}, []
+
+    def start(i):
+        return max([free.get(nodes[i][0], 0.0)] + [end[j] + lat for j, lat in deps[i].items()] + [ready.get(k, 0) for k in nodes[i][2]])
+
+    while cand:
+        best = None
+        for q in sorted(set(nodes[i][0] for i in cand)):
+            c = sorted((i for i in cand if nodes[i][0] == q), key=lambda i: (-pri[i], i))
+            pick, limit = c[0], start(c[0])
+            for i in c[1:]:
+                if start(i) + nodes[i][1] <= limit + SLACK and start(i) < start(pick):
+                    pick, limit = i, min(limit, start(i) + nodes[i][1])
+            if best is None or start(pick) < best[0]:
+                best = (start(pick), pick)
+        st, i = best
+        end[i] = free[nodes[i][0]] = st + nodes[i][1]
+        order.append(i)
+        cand.remove(i)
+        for j in succ[i]:
+            left[j] -= 1
+            if not left[j]:
+                cand.append(j)
+    return order
 
 
 def rank_program(g, core, T, topo):
@@ -30,9 +90,9 @@ def rank_program(g, core, T, topo):
     N = len(T.cores)
     Q = {"v": g.vector, "s": g.scalar, "p": g.tensor, "g": g, "y": g.sync}
     CSEM = {"v": "cv", "s": "cs", "p": "cp", "g": "cg"}
-    count = {"cv": 0, "cs": 0, "cp": 0, "cg": 0, "snd": 0, "outs": 0, "wa0": 0, "wa1": 0, "wa2": 0, "wa3": 0}
+    count = {"cv": 0, "cs": 0, "cp": 0, "cg": 0, "snd": 0, "outs": 0}
     waited = {q: {} for q in Q}
-    writer, readers = {}, {}
+    writer, readers, nodes, ready = {}, {}, [], {}
 
     def need(q, reads, writes):
         ev = {}
@@ -56,71 +116,79 @@ def rank_program(g, core, T, topo):
             writer[k] = ev
             readers[k] = {}
 
-    def op(q, fn, reads, writes):
-        need(q, reads, writes)
-        s = CSEM[q]
-        fn().then_inc(T.sem[s], 1)
-        count[s] += 1
-        note((s, count[s]), reads, writes)
+    def op(q, fn, reads, writes, cost):
+        def issue():
+            need(q, reads, writes)
+            s = CSEM[q]
+            fn().then_inc(T.sem[s], 1)
+            count[s] += 1
+            note((s, count[s]), reads, writes)
+        nodes.append((q, cost, reads, writes, issue, None))
 
-    def load(q, sem, total, out, in_, writes):
+    def load(q, sem, total, out, in_, writes, at):
         Q[q].dma_start(out, in_).then_inc(T.sem[sem], 16)
         note((sem, total), [], writes)
+        for k in writes:
+            ready[k] = at
 
     def store(q, out, in_, reads):
-        need(q, reads, [])
-        Q[q].dma_start(out, in_).then_inc(T.sem.outs, 16)
-        count["outs"] += 16
+        def issue():
+            need(q, reads, [])
+            Q[q].dma_start(out, in_).then_inc(T.sem.outs, 16)
+            count["outs"] += 16
+        nodes.append((q, 60, reads, [], issue, None))
 
     V = g.vector
 
-    def tt(o, a, b, o_, r, w):
-        op("v", lambda: V.tensor_tensor(o, a, b, o_), r, w)
+    def tt(o, a, b, o_, r, w, c=65):
+        op("v", lambda: V.tensor_tensor(o, a, b, o_), r, w, c)
 
     def ts(o, a, s1, s2, o0, o1, r, w):
         if o1 is None:
-            op("v", lambda: V.tensor_scalar(o, a, s1, None, o0), r, w)
+            op("v", lambda: V.tensor_scalar(o, a, s1, None, o0), r, w, 55)
         else:
-            op("v", lambda: V.tensor_scalar(o, a, s1, s2, o0, o1), r, w)
+            op("v", lambda: V.tensor_scalar(o, a, s1, s2, o0, o1), r, w, 55)
 
-    def cp(o, a, r, w):
-        op("v", lambda: V.tensor_copy(o, a), r, w)
+    def cp(o, a, r, w, c=55):
+        op("v", lambda: V.tensor_copy(o, a), r, w, c)
 
-    def tr(o, a, r, w):
-        op("v", lambda: V.transpose(o, a), r, w)
+    def tr(o, a, r, w, c=55):
+        op("v", lambda: V.transpose(o, a), r, w, c)
 
     def ms(o, c, w):
-        op("v", lambda: V.memset(o, c), [], w)
+        op("v", lambda: V.memset(o, c), [], w, 90)
 
-    def scan(o, a, b, init, o0, o1, r, w):
-        op("v", lambda: V.tensor_tensor_scan(o, a, b, init, o0, o1), r, w)
+    def scan(o, a, b, init, o0, o1, r, w, c=100):
+        op("v", lambda: V.tensor_tensor_scan(o, a, b, init, o0, o1), r, w, c)
 
     def quant(q, s, a, r, w):
-        op("v", lambda: V.quantize_mx(q, s, a), r, w)
+        op("v", lambda: V.quantize_mx(q, s, a), r, w, 125)
 
-    def act(o, a, r, w, func=AF.Copy, **kw):
-        op("s", lambda: g.scalar.activation(o, a, func, **kw), r, w)
+    def act(o, a, r, w, func=AF.Copy, c=106, **kw):
+        op("s", lambda: g.scalar.activation(o, a, func, **kw), r, w, c)
 
     def iota(o, pat, base, cm, w, flt=False):
         if flt:
-            op("g", lambda: g.iota(o, pat, base, cm, allow_small_or_imprecise_dtypes=True), [], w)
+            op("g", lambda: g.iota(o, pat, base, cm, allow_small_or_imprecise_dtypes=True), ["sent0"], w, 340)
         else:
-            op("g", lambda: g.iota(o, pat, base, cm), [], w)
+            op("g", lambda: g.iota(o, pat, base, cm), [], w, 140)
 
     bank = [0]
 
     def mm(n, lq, lsc, rq, rsc, r):
         b = bank[0] % 8
         bank[0] += 1
-        op("p", lambda: g.tensor.matmul_mx(T.ps[:, 512 * b:512 * b + n], lq, lsc, rq, rsc, True, True), r, ["ps%d" % b])
+        op("p", lambda: g.tensor.matmul_mx(T.ps[:, 512 * b:512 * b + n], lq, lsc, rq, rsc, True, True), r, ["ps%d" % b], 0.6 * n + 10)
         return b
 
-    def send(t, out, in_, sem, reads):
-        dst = T.cores[(rank + STEP[t]) % N]
-        rid, pid = topo.addr(dst)[0:2]
-        need("g", reads, [])
-        g.remote_dma(out, in_, T.sem[sem], T.sem.snd, pid, rid, topo.mask(core, dst))
-        count["snd"] += len(topo.engines(core, dst))
+    def send(t, out, in_, sem, reads, key, lat, w=()):
+        def issue():
+            dst = T.cores[(rank + STEP[t]) % N]
+            rid, pid = topo.addr(dst)[0:2]
+            need("g", reads, [])
+            g.remote_dma(out, in_, T.sem[sem], T.sem.snd, pid, rid, topo.mask(core, dst))
+            count["snd"] += len(topo.engines(core, dst))
+        nodes.append(("g", 500, reads, ["sends"] + list(w), issue, (key, lat)))
 
     def arriving(t):
         return len(topo.engines(T.cores[(rank - STEP[t]) % N], core))
@@ -129,44 +197,43 @@ def rank_program(g, core, T, topo):
         for h in range(2):
             writer["land%d_%d" % (t, h)] = ("ar%d_%d" % (t, h), 2 * arriving(t))
         writer["ll%d" % t] = ("al%d" % t, arriving(t))
-    writer["land0_0"] = writer["land0_1"] = ("ar0_0", 3 * arriving(0))
+    writer["land0_0"] = ("ar0_0", 3 * arriving(0))
 
-    def send_codes(t, m0, m1, sem):
-        send(t, T["lc%d" % t][:, 128 * m0:128 * m1].bitcast(dt.uint8), T["qt%d" % t][:, 128 * m0:128 * m1].bitcast(dt.uint8), sem,
-             ["qt%d_%d" % (t, m) for m in range(m0, m1)])
+    def send_codes(t, m0, m1, h):
+        send(t, T["lc%d" % t][:, 128 * m0:128 * m1].bitcast(dt.uint8), T["qt%d" % t][:, 128 * m0:128 * m1].bitcast(dt.uint8), "ar%d_%d" % (t, h),
+             ["qt%d_%d" % (t, m) for m in range(m0, m1)], "land%d_%d" % (t, h), FAR)
 
-    def send_scales(t, m0, m1, sem):
-        send(t, T["ls%d" % t][:, 128 * m0:128 * m1], T["st%d" % t][:, 128 * m0:128 * m1], sem, ["qt%d_%d" % (t, m) for m in range(m0, m1)])
-
-    def send_half(t, h):
-        send_codes(t, 2 * h, 2 * h + 2, "ar%d_%d" % (t, h))
-        send_scales(t, 2 * h, 2 * h + 2, "ar%d_%d" % (t, h))
+    def send_scales(t, m0, m1, h):
+        send(t, T["ls%d" % t][:, 128 * m0:128 * m1], T["st%d" % t][:, 128 * m0:128 * m1], "ar%d_%d" % (t, h),
+             ["qt%d_%d" % (t, m) for m in range(m0, m1)], "land%d_%d" % (t, h), FAR)
 
     def pk(t, m):
         return ["tc%d_%d_0" % (t, m), "tc%d_%d_1" % (t, m)]
 
     for m in range(4):
-        load("y", "x%d" % m, 16, T.tc0[:, 512 * m:512 * m + 512], T.x[:, 512 * m:512 * m + 512], pk(0, m))
-    load("s", "lu", 16, T.us[:], T.u[:], ["us"])
-    load("s", "lp", 144, T.pi[:, 0:32], T.p[:], ["pi"])
+        load("y", "x%d" % m, 16, T.tc0[:, 512 * m:512 * m + 512], T.x[:, 512 * m:512 * m + 512], pk(0, m), 2500 + 400 * m)
+    load("s", "lu", 16, T.us[:], T.u[:], ["us"], 2300)
+    load("s", "lp", 144, T.pi[:, 0:32], T.p[:], ["pi"], 3500)
     for a in range(4):
         for h in range(2):
-            load("s", "lp", 144, T.pi[32 * a:32 * a + 32, 32 + 16 * h:48 + 16 * h], T.p[32 * a + 16 * h:32 * a + 16 * h + 16, :], ["pi"])
-    load("s", "lw", 32, T.qw[:].bitcast(dt.uint8), T.wc[:], ["w"])
-    load("s", "lw", 32, T.sw[:], T.ws[:], ["w"])
-    load("s", "lv", 16, T.vs[:], T.v[:], ["vs"])
+            load("s", "lp", 144, T.pi[32 * a:32 * a + 32, 32 + 16 * h:48 + 16 * h], T.p[32 * a + 16 * h:32 * a + 16 * h + 16, :], ["pi"], 3500)
+    load("s", "lw", 32, T.qw[:].bitcast(dt.uint8), T.wc[:], ["w"], 5000)
+    load("s", "lw", 32, T.sw[:], T.ws[:], ["w"], 5000)
+    load("s", "lv", 16, T.vs[:], T.v[:], ["vs"], 20000)
 
     iota(T.ip[:], [[0, 4]], 0, 1, ["ip"])
     iota(T.cb[:], [[4, 4]], 0, 0, ["cb"])
     ms(T.ones[:], 1.0, ["ones"])
-    op("g", lambda: g.affine_select(T.zt[:], T.ones[:], [[-1, 520]], A.is_equal, 0.0, 3, 4), ["ones"], ["zt"])
+    op("g", lambda: g.affine_select(T.zt[:], T.ones[:], [[-1, 520]], A.is_equal, 0.0, 3, 4), ["ones", "ip", "cb"], ["zt"], 1030)
     iota(T.iq[:], [[4, 32]], 0, 0, ["iq"])
-    ms(T.k0[:], SENT, ["k0"])
+    ms(T.k0[:], SENT, ["k0_0", "k0_1"])
     ms(T.ko[:], SENT, ["ko"])
     ms(T.d0[:], 0.0, ["right", "on"])
     ms(T.dk[:], 0.0, ["wn", "pk"])
-    ms(T.gg[:], 1.0, ["g0", "g1", "g2", "gc"])
+    ms(T.e0[:], 0.0, ["ond", "nonr"])
+    ms(T.gg[:], 1.0, ["g0", "g1", "g2", "gc", "gc2"])
     ms(T.cd[:], -1.0e9, ["cd"])
+    ms(T.dk[:, 118:150:3], SENT, ["wn"])
     ms(T.gg[:, 0:4], 0.0, ["gc"])
     ms(T.gg[:, 5:9], 0.0, ["gc2"])
     ms(T.cd[:, 0:120:3], 1.0e9, ["cd"])
@@ -178,9 +245,10 @@ def rank_program(g, core, T, topo):
     ts(col[:, 4:8], sm[:, 16:20], 48.0, 6168.0, A.mult, A.add, ["sj"], ["yb0"])
     tt(sm[:, 4:8], sm[:, 0:4], T.cb[:], A.add, ["sr", "cb"], ["sm"])
     cp(col[:, 0:1], sm[:, 20:21], ["st"], ["tcol"])
-    act(T.jb[:, 0:3 * JS], T.ones[:, 0:3 * JS], ["ones", "m3"], ["j0", "j1", "j2", "tu0", "tu1", "tu2"], AF.Identity, bias=col[:, 1:2], scale=0.0)
-    act(T.ptp[:], T.ones[:, 0:50], ["ones", "m3"], ["ptp0", "ptp1"], AF.Identity, bias=col[:, 1:2], scale=0.0)
-    act(T.jb[:, 3 * JS:6 * JS], T.ones[:, 0:3 * JS], ["ones", "m3"], ["j3", "j4", "j5", "tu3", "tu4", "tu5"], AF.Identity, bias=col[:, 1:2], scale=0.0)
+    jk = lambda z: ["j%d" % z, "t%d" % z, "u%d" % z]
+    act(T.jb[:, 0:3 * JS], T.ones[:, 0:3 * JS], ["ones", "m3"], jk(0) + jk(1) + jk(2), AF.Identity, 380, bias=col[:, 1:2], scale=0.0)
+    act(T.ptp[:], T.ones[:, 0:50], ["ones", "m3"], ["ptp0", "ptp1"], AF.Identity, 55, bias=col[:, 1:2], scale=0.0)
+    act(T.jb[:, 3 * JS:6 * JS], T.ones[:, 0:3 * JS], ["ones", "m3"], jk(3) + jk(4) + jk(5), AF.Identity, 380, bias=col[:, 1:2], scale=0.0)
     ts(sm[:, 21:22], sm[:, 0:1], 10.0, None, A.mult, None, ["sr"], ["s10"])
     ts(sm[:, 24:25], sm[:, 0:1], 1.0, None, A.min, None, ["sr"], ["smin"])
     ts(sm[:, 8:12], sm[:, 4:8], 43.0, None, A.mult, None, ["sm"], ["si"])
@@ -201,42 +269,18 @@ def rank_program(g, core, T, topo):
 
     def tu(s):
         o = s * JS
-        tt(T.jb[:, o:o + 117:3], T.jb[:, o + 5:o + 122:3], T.jb[:, o + 32:o + 149:3], A.subtract, ["j%d" % s], ["t%d" % s, "tu%d" % s])
+        tt(T.jb[:, o:o + 117:3], T.jb[:, o + 5:o + 122:3], T.jb[:, o + 32:o + 149:3], A.subtract, ["j%d" % s], ["t%d" % s])
 
     def uu(s):
         o = s * JS
         tt(T.jb[:, o + 1:o + 118:3], T.jb[:, o + 32:o + 149:3], T.jb[:, o + 2:o + 119:3], A.subtract, ["j%d" % s], ["u%d" % s])
 
     def first_ids(s, pt, key):
-        return [lambda: ts(T.ptp[:, 0:4, 0:4], pt[:, 0:16], 4.0, None, A.mult, None, [key], ["ptp0"]),
-                lambda: ts(T.ptp[:, 0:4, 5:9], pt[:, 16:32], 4.0, None, A.mult, None, [key], ["ptp1"]),
-                lambda: cp(T.jb[:, s * JS + 2:s * JS + 150:3], T.ptp[:], ["ptp0", "ptp1"], ["j%d" % s]),
-                lambda: tu(s), lambda: uu(s)]
-
-    pi = T.pi[:, 0:66]
-    later = [
-        lambda: ts(T.w1[:], pi, 3, None, A.bitwise_and, None, ["pi", "pi2"], ["w1"]),
-        lambda: ts(T.w2[:], pi, 2, 3, A.arith_shift_right, A.bitwise_and, ["pi", "pi2"], ["w2"]),
-        lambda: ts(T.w3[:], pi, 2, 124, A.arith_shift_right, A.bitwise_and, ["pi", "pi2"], ["w3"]),
-        lambda: ts(T.w4[:], T.w1[:], 3.0, None, A.is_equal, None, ["w1"], ["w4"]),
-        lambda: ts(T.w5[:], T.w2[:], -2.0, 9.0, A.mult, A.add, ["w2"], ["w5"]),
-        lambda: ts(T.w2[:], T.w2[:], 3.0, None, A.mult, None, ["w2"], ["w2"]),
-        lambda: tt(T.w4[:], T.w4[:], T.w5[:], A.mult, ["w4", "w5"], ["w4"]),
-        lambda: tt(T.w1[:], T.w1[:], T.w2[:], A.add, ["w1", "w2"], ["w1"]),
-        lambda: tt(T.w1[:], T.w1[:], T.w4[:], A.add, ["w1", "w4"], ["w1"]),
-        lambda: ts(T.w2[:], T.w1[:], 2, None, A.arith_shift_right, None, ["w1"], ["w2"]),
-        lambda: tt(T.w3[:], T.w3[:], T.w1[:], A.add, ["w1", "w3"], ["w3"]),
-        lambda: ts(T.w2[:], T.w2[:], 124.0, None, A.mult, None, ["w2"], ["w2"]),
-        lambda: tt(T.pf2[:], T.w3[:], T.w2[:], A.add, ["w2", "w3"], ["pf2"]),
-        lambda: tr(T.pt2[:], T.pf2[:, 0:64], ["pf2"], ["pt2"]),
-        lambda: ts(T.posl[:], T.iq[:], T.pf2[:, 64:65], None, A.add, None, ["pf2", "iq"], ["posl"]),
-        lambda: cp(T.ob[:], T.pt2[:, 32:64], ["pt2"], ["ob"]),
-    ] + first_ids(1, T.pt2, "pt2")
-
-    def some(n):
-        for _ in range(n):
-            if later:
-                later.pop(0)()
+        ts(T.ptp[:, 0:4, 0:4], pt[:, 0:16], 4.0, None, A.mult, None, [key], ["ptp0"])
+        ts(T.ptp[:, 0:4, 5:9], pt[:, 16:32], 4.0, None, A.mult, None, [key], ["ptp1"])
+        cp(T.jb[:, s * JS + 2:s * JS + 150:3], T.ptp[:], ["ptp0", "ptp1"], ["j%d" % s])
+        tu(s)
+        uu(s)
 
     def key_piece(t, m):
         return mm(128, T.qu[:], T.su[:], T["qt%d" % t][:, 128 * m:128 * m + 128], T["st%d" % t][:, 128 * m:128 * m + 128], ["qu", "qt%d_%d" % (t, m)])
@@ -251,206 +295,176 @@ def rank_program(g, core, T, topo):
     for b in range(4):
         quant(T.qe[:, 128 * b:128 * b + 128], T.se[:, 128 * b:128 * b + 128], T.zt[:, 3 - b:515 - b], ["zt"], ["e%d" % b])
     quant(T.qu[:], T.su[:], T.us[:], ["us"], ["qu"])
-    ids0 = first_ids(0, T.pt, "pt")
+    quant(T.qv[:], T.sv[:], T.vs[:], ["vs"], ["qv"])
     for m in range(4):
         qt_piece(0, m)
         key_copy(m, key_piece(0, m))
-        if m == 0:
-            send_codes(0, 0, 1, "ar0_0")
-        if m == 1:
-            cp(T.pf[:], T.pi[:, 0:64], ["pi"], ["pf"])
-        if m == 2:
-            tr(T.pt[:], T.pf[:], ["pf"], ["pt"])
-        if m == 3:
-            send_codes(0, 1, 4, "ar0_0")
-            send_scales(0, 0, 4, "ar0_0")
-            cp(T.oa[:], T.pt[:, 32:64], ["pt"], ["oa"])
-            ids0[0]()
-            ids0[1]()
-    later[0:0] = ids0[2:]
+    send_codes(0, 0, 1, 0)
+    send_codes(0, 1, 4, 0)
+    send_scales(0, 0, 4, 0)
+    cp(T.pf[:], T.pi[:, 0:64], ["pi"], ["pf"])
+    tr(T.pt[:], T.pf[:], ["pf"], ["pt"])
+    cp(T.oa[:], T.pt[:, 32:64], ["pt"], ["oa"])
+    first_ids(0, T.pt, "pt")
+
+    def positions():
+        pi, r = T.pi[:, 0:66], ["pi", "pi2", "oa"]
+        ts(T.w1[:], pi, 3, None, A.bitwise_and, None, r, ["w1"])
+        ts(T.w2[:], pi, 2, 3, A.arith_shift_right, A.bitwise_and, r, ["w2"])
+        ts(T.w3[:], pi, 2, 124, A.arith_shift_right, A.bitwise_and, r, ["w3"])
+        ts(T.w4[:], T.w1[:], 3.0, None, A.is_equal, None, ["w1"], ["w4"])
+        ts(T.w5[:], T.w2[:], -2.0, 9.0, A.mult, A.add, ["w2"], ["w5"])
+        ts(T.w2[:], T.w2[:], 3.0, None, A.mult, None, ["w2"], ["w2"])
+        tt(T.w4[:], T.w4[:], T.w5[:], A.mult, ["w4", "w5"], ["w4"], 110)
+        tt(T.w1[:], T.w1[:], T.w2[:], A.add, ["w1", "w2"], ["w1"], 110)
+        tt(T.w1[:], T.w1[:], T.w4[:], A.add, ["w1", "w4"], ["w1"], 110)
+        ts(T.w2[:], T.w1[:], 2, None, A.arith_shift_right, None, ["w1"], ["w2"])
+        tt(T.w3[:], T.w3[:], T.w1[:], A.add, ["w1", "w3"], ["w3"], 110)
+        ts(T.w2[:], T.w2[:], 124.0, None, A.mult, None, ["w2"], ["w2"])
+        tt(T.pf2[:], T.w3[:], T.w2[:], A.add, ["w2", "w3"], ["pf2"], 110)
+        tr(T.pt2[:], T.pf2[:, 0:64], ["pf2"], ["pt2"])
+        ts(T.posl[:], T.iq[:], T.pf2[:, 64:65], None, A.add, None, ["pf2", "iq"], ["posl"])
+        cp(T.ob[:], T.pt2[:, 32:64], ["pt2"], ["ob"])
+        first_ids(1, T.pt2, "pt2")
 
     ssb_keys = ["ssb%d" % m for m in range(4)]
+    gk = ["g0", "g1", "g2"]
+    k0k = ["k0_0", "k0_1"]
 
-    for t in range(3):
+    def one_round(t):
         tc, nx = T["tc%d" % t], T["tc%d" % (t + 1)]
         tck = [k for m in range(4) for k in pk(t, m)]
         ok, okk = (T.oa, "oa") if t == 0 else (T.ob, "ob")
-        some(1)
-        cp(T.kr[:, 0:128], T.ssb[:].indirect(ok[:, 0:8]), ssb_keys + [okk], ["kr0"])
+        cp(T.kr[:, 0:128], T.ssb[:].indirect(ok[:, 0:8]), ssb_keys + [okk], ["kr0"], 215)
         for i in range(1, 4):
-            act(T.kr[:, 128 * i:128 * i + 128], T.ssb[:].indirect(ok[:, 8 * i:8 * i + 8]), ssb_keys + [okk], ["kr%d" % i])
+            act(T.kr[:, 128 * i:128 * i + 128], T.ssb[:].indirect(ok[:, 8 * i:8 * i + 8]), ssb_keys + [okk], ["kr%d" % i], c=230)
         for i in range(4):
-            if i != 1:
-                some(1)
-            tr(T.tp[:, 128 * i:128 * i + 128], T.kr[:, 128 * i:128 * i + 128], ["kr%d" % i], ["tp%d" % i])
-        some(1)
+            tr(T.tp[:, 128 * i:128 * i + 128], T.kr[:, 128 * i:128 * i + 128], ["kr%d" % i], ["tp%d" % i], 106)
         for h in range(2):
-            cp(T.k0[:, 0:4, 5 * h:5 * h + 4], T.tp[:, 16 * h:512:32], ["tp0", "tp1", "tp2", "tp3"], ["k0_%d" % h] + (["k0"] if h == 0 else []))
-        some(1)
-
-        def unpack(h):
+            cp(T.k0[:, 0:4, 5 * h:5 * h + 4], T.tp[:, 16 * h:512:32], ["tp0", "tp1", "tp2", "tp3"], ["k0_%d" % h])
+        for h in range(2):
             for b in range(4):
                 bk = mm(256, T.qe[:, 128 * b:128 * b + 128], T.se[:, 128 * b:128 * b + 128], T["lc%d" % t][:, 256 * h:256 * h + 256],
-                        T["ls%d" % t][:, 256 * h:256 * h + 256], ["e%d" % b, "land%d_%d" % (t, h)])
-                act(T.dd[:, 1024 * h + b:1024 * h + 1024:4], T.ps[:, 512 * bk:512 * bk + 256], ["ps%d" % bk], ["dd%d_%d" % (h, b)])
+                        T["ls%d" % t][:, 256 * h:256 * h + 256], ["e%d" % b, "land%d_%d" % (t, h if t else 0)])
+                act(T.dd[:, 1024 * h + b:1024 * h + 1024:4], T.ps[:, 512 * bk:512 * bk + 256], ["ps%d" % bk, "kr3"], ["dd%d_%d" % (h, b)], c=212)
 
-        def mark(k):
-            o = (k + 2) * JS
-            act(T.yy[:, k:117:3], T.jb[:, o + 2:o + 119:3], ["j%d" % (k + 2), "t%d" % (k + 2), "u%d" % (k + 2), "yb"], ["yy%d" % k], AF.Identity,
-                bias=col[:, 8 + k:9 + k], scale=-2.0)
-
-        unpack(0)
+        tt(T.d0[:, 1:120:3], T.k0[:, 0:4, 1:11], T.k0[:, 1:5, 0:10], A.is_ge, k0k, ["right"])
         for k in range(4):
             s = (0 if t == 0 else 1) if k == 0 else k + 1
             so = k + 2
             if k == 0:
-                kc, kr_, kd, n, kk = T.k0[:, 0:4, 0:10], T.k0[:, 0:4, 1:11], T.k0[:, 1:5, 0:10], 40, ["k0", "k0_0", "k0_1"]
+                kc, kr_, kd, n, kk = T.k0[:, 0:4, 0:10], T.k0[:, 0:4, 1:11], T.k0[:, 1:5, 0:10], 40, k0k
             else:
                 kc, kr_, kd, n, kk = T.ko[:, 2:119:3], T.ko[:, 5:122:3], T.ko[:, 32:149:3], 39, ["ko"]
-            jin = ["right", "on", "j%d" % s, "t%d" % s, "u%d" % s]
-            jout = ["j%d" % so, "t%d" % so, "u%d" % so, "tu%d" % so]
-            tt(T.d0[:, 1:3 * n:3], kr_, kd, A.is_ge, kk, ["right"])
+                cp(T.d0[:, 1:117:3], T.rr[:, 2:117:3], ["rr"], ["right"])
+            for i in range(3):
+                d = T.d0[:, 30 * i + 1:30 * i + 30:3] if k == 0 else T.rr[:, 30 * i + 2:30 * i + 30:3]
+                scan(T.gg[:, 10 * i + 10:10 * i + 20], d, T.gg[:, 10 * i:10 * i + 10], 1.0, A.mult, A.max,
+                     ["right" if k == 0 else "rr", "gc", "gc2"] + gk[max(i - 1, 0):i], ["g%d" % i], 55)
             if k < 3:
                 tt(T.dk[:, 1:3 * n:3], kr_, kd, A.max, kk, ["wn"])
-            else:
-                uu(s)
-            for i in range(3):
-                scan(T.gg[:, 10 * i + 10:10 * i + 20], T.d0[:, 30 * i + 1:30 * i + 30:3], T.gg[:, 10 * i:10 * i + 10], 1.0, A.mult, A.max,
-                     ["right", "gc", "gc2"] + (["g%d" % (i - 1)] if i else []), ["g%d" % i])
-                if 0 < k < 3 and i == 0:
-                    uu(s)
-                elif k == 2 and i == 1:
-                    scan(T.jb[:, so * JS:so * JS + 18], T.d0[:, 0:18], T.jb[:, s * JS:s * JS + 18], 0.0, A.mult, A.add, jin, jout)
-                elif k == 2:
-                    c0 = 8 if t == 0 else 10
-                    slabs = [x % z for x in ("j%d", "t%d", "u%d") for z in range(5)]
-                    cp(T.lf[:], T.jb[:, 0:5 * JS].indirect(T.lst[:, c0:c0 + 2]), slabs + ["lfa0", "lfa1", "lfb0", "lfb1"], ["lf"])
-                else:
-                    some(1)
-            if k > 0:
-                if k == 2:
-                    unpack(1)
-                mark(k - 1)
-            gk = ["g0", "g1", "g2"]
-            if k < 3:
-                tt(T.non[:, 0:n], T.gg[:, 9:9 + n], T.gg[:, 0:n], A.is_le, gk, ["non"])
+                tt(T.e1[:, 2:3 * n:3], T.dk[:, 4:3 * n + 3:3], kd, A.is_ge, kk + ["wn"], ["c10"])
+                tt(T.c01[:, 0:n], kr_, T.dk[:, 31:3 * n + 30:3], A.is_ge, kk + ["wn"], ["c01"])
+                tt(T.e1[:, 1:3 * n:3], T.d0[:, 1:3 * n:3], T.e1[:, 2:3 * n:3], A.subtract, ["right", "c10"], ["ed"])
+                tt(T.e1[:, 0:3 * n:3], T.c01[:, 0:n], T.d0[:, 1:3 * n:3], A.subtract, ["right", "c01"], ["eb"])
             if k == 2:
+                scan(T.jb[:, 4 * JS:4 * JS + 18], T.d0[:, 0:18], T.jb[:, 3 * JS:3 * JS + 18], 0.0, A.mult, A.add, ["right", "on"] + jk(3), jk(4), 55)
+                c0 = 8 if t == 0 else 10
+                cp(T.lf[:], T.jb[:, 0:5 * JS].indirect(T.lst[:, c0:c0 + 2]), [x for z in range(5) for x in jk(z)] + ["lfa0", "lfa1", "lfb0", "lfb1"], ["lf"], 92)
                 tr(T.lft[:], T.lf[:], ["lf"], ["lft"])
-            tt(T.d0[:, 2:117:3], T.gg[:, 9:48], T.gg[:, 0:39], A.is_gt, gk, ["on"])
-            if k == 2:
                 ts(T["sl%d" % t][:], T.lft[:], col[:, 0:1], None, A.add, None, ["lft", "tcol"], ["sl%d" % t])
-                send(t, T["ll%d" % t][:], T["sl%d" % t][:], "al%d" % t, ["sl%d" % t])
+                send(t, T["ll%d" % t][:], T["sl%d" % t][:], "al%d" % t, ["sl%d" % t], "ll%d" % t, FARL, ["sent0"] if t == 0 else [])
             if k < 3:
+                tt(T.e0[:, 1:117:3], T.gg[:, 19:58], T.gg[:, 10:49], A.is_gt, gk, ["ond"])
+                tt(T.e0[:, 2:117:3], T.gg[:, 10:49], T.gg[:, 1:40], A.is_le, gk, ["nonr"])
+                scan(T.rr[:, 0:117], T.e0[:, 0:117], T.e1[:, 0:117], 0.0, A.mult, A.add, ["ond", "nonr", "c10", "ed", "eb"], ["rr"])
+            tt(T.d0[:, 2:117:3], T.gg[:, 9:48], T.gg[:, 0:39], A.is_gt, gk, ["on"])
+            if k < 2:
+                tt(T.non[:, 0:n], T.gg[:, 9:9 + n], T.gg[:, 0:n], A.is_le, gk, ["non"])
                 tt(T.dk[:, 2:3 * n:3], T.non[:, 0:n], kc, A.mult, kk + ["non"], ["pk"])
-            scan(T.jb[:, so * JS:so * JS + 117], T.d0[:, 0:117], T.jb[:, s * JS:s * JS + 117], 0.0, A.mult, A.add, jin, jout)
-            if k < 3:
                 scan(T.ko[:, 0:117], T.d0[:, 0:117], T.dk[:, 0:117], 0.0, A.mult, A.add, ["right", "on", "wn", "pk"], ["ko"])
+            scan(T.jb[:, so * JS:so * JS + 117], T.d0[:, 0:117], T.jb[:, s * JS:s * JS + 117], 0.0, A.mult, A.add, ["right", "on"] + jk(s), jk(so))
+            if k < 3:
                 tu(so)
+                uu(so)
+                act(T.yy[:, k:117:3], T.jb[:, so * JS + 2:so * JS + 119:3], jk(so) + ["yb"], ["yy%d" % k], AF.Identity, 55, bias=col[:, 8 + k:9 + k], scale=-2.0)
+        if t == 0:
+            positions()
 
         win = T.jb[:, 5 * JS:6 * JS]
-
-        def lists(hf):
-            cp(T.in2[:, 64 * hf:64 * hf + 64], win.indirect(T.lst[:, 4 * hf:4 * hf + 4]), ["j5", "t5", "u5", "la0", "la1"], ["in2_%d" % hf])
-            tr(T.in2t[:, 64 * hf:64 * hf + 64], T.in2[:, 64 * hf:64 * hf + 64], ["in2_%d" % hf], ["in2t%d" % hf])
-            ts(T.off[:, 64 * hf:64 * hf + 64], T.in2t[:, 64 * hf:64 * hf + 64], col[:, 0:1], None, A.add, None, ["in2t%d" % hf, "tcol"], ["off%d" % hf])
-
-        def gather(q, m, c0, c1):
-            w = tc[:, 0:2048] if m < 2 else tc[:, 0:2560]
-            r = tck + ["off%d" % (m // 2)] + ([] if m < 2 else ["fd%d" % t])
-            o = nx[:, 512 * m + 16 * c0:512 * m + 16 * c1]
-            (cp if q == "v" else act)(o, w.indirect(T.off[:, 32 * m + c0:32 * m + c1]), r, pk(t + 1, m)[c0 // 16:c1 // 16])
-
-        def qv(m):
-            quant(T.qz[:, 128 * m:128 * m + 128], T.sz[:, 128 * m:128 * m + 128], nx[:, 512 * m:512 * m + 512], pk(t + 1, m), ["qz%d" % m])
-            return [mm(128, T.qw[:, 128 * b:128 * b + 128], T.sw[:, 128 * b:128 * b + 128], T.qz[:, 128 * m:128 * m + 128],
-                       T.sz[:, 128 * m:128 * m + 128], ["w", "qz%d" % m]) for b in range(4)]
-
-        def relu(m, banks):
-            for b in range(4):
-                act(T.a32[:, 512 * m + b:512 * m + 512:4], T.ps[:, 512 * banks[b]:512 * banks[b] + 128], ["ps%d" % banks[b]], ["a%d_%d" % (m, b)],
-                    AF.Relu, scale=0.015625)
-
         bk, sk = {}, {}
-
-        def step(name):
+        for name in ORDER.split():
             k, m = name[0:2], int(name[2:] or 0)
             ak = ["a%d_%d" % (m, b) for b in range(4)]
             piece = nx[:, 512 * m:512 * m + 512]
             if k == "L_":
-                lists(m)
+                c = slice(64 * m, 64 * m + 64)
+                cp(T.in2[:, c], win.indirect(T.lst[:, 4 * m:4 * m + 4]), jk(5) + ["la0", "la1"], ["in2_%d" % m], 133)
+                tr(T.in2t[:, c], T.in2[:, c], ["in2_%d" % m], ["in2t%d" % m])
+                ts(T.off[:, c], T.in2t[:, c], col[:, 0:1], None, A.add, None, ["in2t%d" % m, "tcol"], ["off%d" % m])
             elif k[0] == "G":
-                q, c0, c1 = {"Ga": ("v", 0, 16), "Gb": ("s", 16, 32), "Gc": ("s", 0, 16), "Gd": ("v", 16, 32), "Gs": ("s", 0, 32), "Gv": ("v", 0, 32)}[k]
-                gather(q, m, c0, c1)
+                q, hf = {"Ga": (cp, 0), "Gb": (act, 1), "Gc": (act, 0), "Gd": (cp, 1)}[k]
+                w = tc[:, 0:2048] if m < 2 else tc[:, 0:2560]
+                q(nx[:, 512 * m + 256 * hf:512 * m + 256 * hf + 256], w.indirect(T.off[:, 32 * m + 16 * hf:32 * m + 16 * hf + 16]),
+                  tck + ["off%d" % (m // 2)] + ([] if m < 2 else ["fd%d" % t]), pk(t + 1, m)[hf:hf + 1], c=390)
             elif k == "QV":
-                bk[m] = qv(m)
+                c = slice(128 * m, 128 * m + 128)
+                quant(T.qz[:, c], T.sz[:, c], piece, pk(t + 1, m), ["qz%d" % m])
+                bk[m] = [mm(128, T.qw[:, 128 * b:128 * b + 128], T.sw[:, 128 * b:128 * b + 128], T.qz[:, c], T.sz[:, c], ["w", "qz%d" % m]) for b in range(4)]
             elif k == "R_":
-                relu(m, bk[m])
+                for b in range(4):
+                    act(T.a32[:, 512 * m + b:512 * m + 512:4], T.ps[:, 512 * bk[m][b]:512 * bk[m][b] + 128], ["ps%d" % bk[m][b]], [ak[b]],
+                        AF.Relu, scale=0.015625)
             elif k == "A_":
-                tt(piece, T.a32[:, 512 * m:512 * m + 512], piece, A.add, ak + pk(t + 1, m), pk(t + 1, m))
-            elif k == "D_":
-                need("g", ak, pk(t + 1, m))
-                g.dma_start(piece, T.a32[:, 512 * m:512 * m + 512], accum_op=A.add).then_inc(T.sem["wa%d" % m], 16)
-                count["wa%d" % m] += 16
-                note(("wa%d" % m, count["wa%d" % m]), ak, pk(t + 1, m))
+                tt(piece, T.a32[:, 512 * m:512 * m + 512], piece, A.add, ak + pk(t + 1, m), pk(t + 1, m), 850)
             elif k == "QT":
                 qt_piece(t + 1, m)
                 if t < 2:
                     sk[m] = key_piece(t + 1, m)
-            elif k == "SC":
-                if t < 2:
-                    key_copy(m, sk[m])
-            elif k == "SH":
-                if t < 2:
-                    send_half(t + 1, m)
+            elif k == "SC" and t < 2:
+                key_copy(m, sk[m])
+            elif k == "SH" and t < 2:
+                send_codes(t + 1, 2 * m, 2 * m + 2, m)
+                send_scales(t + 1, 2 * m, 2 * m + 2, m)
             elif k == "C0":
                 scan(T.cc[:, 0:117], T.cd[:, 0:117], T.yy[:, 0:117], 0.0, A.max, A.min, ["cd", "yy0", "yy1", "yy2"], ["cc"])
             elif k == "C1":
                 tt(T.jb[:, 5 * JS + 2:5 * JS + 119:3], T.jb[:, 5 * JS + 2:5 * JS + 119:3], T.cc[:, 2:117:3], A.min, ["j5", "cc"], ["j5"])
-            elif k in ("FD", "FV"):
-                (act if k == "FD" else cp)(tc[:, 2048:2560], T.dd[:].indirect(T["ll%d" % t][:]),
-                                           ["dd%d_%d" % (h, b) for h in range(2) for b in range(4)] + ["ll%d" % t], ["fd%d" % t])
-            elif k == "X0":
-                if t == 0:
-                    iota(T.olt[:, 0:128], [[16, 32], [1, 4]], 0, 0, ["olt0"], True)
-                    iota(T.olt[:, 256:384], [[16, 32], [1, 4]], 11, 0, ["olt2"], True)
-                    iota(T.olt[:, 128:256], [[16, 32], [3, 2], [1, 2]], 5, 0, ["olt1"], True)
-                    iota(T.olt[:, 3:128:4], [[16, 32]], 4, 0, ["olt0"], True)
-                if t == 1:
-                    iota(T.olt[:, 256:384:4], [[16, 32]], 10, 0, ["olt2"], True)
-                    iota(T.olt[:, 384:512], [[16, 32], [4, 4]], 3, 0, ["olt3"], True)
-                    iota(T.olt[:, 512:640], [[1, 32], [32, 4]], 512, 0, ["olt4"], True)
-            elif k == "X1":
-                if t == 0:
-                    some(32)
-                if t == 1:
-                    quant(T.qv[:], T.sv[:], T.vs[:], ["vs"], ["qv"])
-                if t == 2:
-                    cp(T.ln[:], win.indirect(T.lst[:, 12:14]), ["j5", "t5", "u5", "lnl0", "lnl1"], ["ln"])
-                    tr(T.lnt[:], T.ln[:], ["ln"], ["lnt"])
-                    ts(T.oln[:], T.lnt[:], 0.25, None, A.mult, None, ["lnt"], ["oln"])
-            elif k == "X2":
-                if t == 2:
-                    act(T.olr[:], T.olt[:].indirect(T.oln[:]), ["oln"] + ["olt%d" % i for i in range(5)], ["olr"])
-                    store("y", T.ol[:], T.olr[0:128:16, :], ["olr"])
+            elif k == "FD":
+                act(tc[:, 2048:2560], T.dd[:].indirect(T["ll%d" % t][:]), ["dd%d_%d" % (h, b) for h in range(2) for b in range(4)] + ["ll%d" % t],
+                    ["fd%d" % t], c=730)
+            elif k == "X0" and t == 0:
+                iota(T.olt[:, 0:128], [[16, 32], [1, 4]], 0, 0, ["olt0"], True)
+                iota(T.olt[:, 256:384], [[16, 32], [1, 4]], 11, 0, ["olt2"], True)
+                iota(T.olt[:, 128:256], [[16, 32], [3, 2], [1, 2]], 5, 0, ["olt1"], True)
+                iota(T.olt[:, 3:128:4], [[16, 32]], 4, 0, ["olt0"], True)
+                iota(T.olt[:, 256:384:4], [[16, 32]], 10, 0, ["olt2"], True)
+                iota(T.olt[:, 384:512], [[16, 32], [4, 4]], 3, 0, ["olt3"], True)
+                iota(T.olt[:, 512:640], [[1, 32], [32, 4]], 512, 0, ["olt4"], True)
+            elif k == "X1" and t == 2:
+                cp(T.ln[:], win.indirect(T.lst[:, 12:14]), jk(5) + ["lnl0", "lnl1"], ["ln"], 92)
+                tr(T.lnt[:], T.ln[:], ["ln"], ["lnt"])
+                ts(T.oln[:], T.lnt[:], 0.25, None, A.mult, None, ["lnt"], ["oln"])
+            elif k == "X2" and t == 2:
+                act(T.olr[:], T.olt[:].indirect(T.oln[:]), ["oln", "a3_3"] + ["olt%d" % i for i in range(5)], ["olr"], c=730)
+                store("y", T.ol[:], T.olr[0:128:16, :], ["olr"])
 
-        for name in ORDER.split():
-            step(name)
+    for t in range(3):
+        one_round(t)
 
     qk = ["qt3_%d" % m for m in range(4)] + ["posl"]
-    banks = []
     for h in range(2):
         lo, hi = 256 * h, 256 * h + 256
-        cp(T.qn[:, lo:hi].bitcast(dt.uint32), T.qt3[:, 0:512].bitcast(dt.uint32).indirect(T.posl[:, 16 * h:16 * h + 16]), qk, ["qn%d" % h])
-        act(T.sn[:, lo:hi], T.st3[:, 0:512].indirect(T.posl[:, 16 * h:16 * h + 16]), qk, ["sn%d" % h])
-        banks.append(mm(256, T.qv[:], T.sv[:], T.qn[:, lo:hi], T.sn[:, lo:hi], ["qv", "qn%d" % h, "sn%d" % h]))
+        cp(T.qn[:, lo:hi].bitcast(dt.uint32), T.qt3[:, 0:512].bitcast(dt.uint32).indirect(T.posl[:, 16 * h:16 * h + 16]), qk, ["qn%d" % h], 390)
+        act(T.sn[:, lo:hi], T.st3[:, 0:512].indirect(T.posl[:, 16 * h:16 * h + 16]), qk, ["sn%d" % h], c=390)
+        b = mm(256, T.qv[:], T.sv[:], T.qn[:, lo:hi], T.sn[:, lo:hi], ["qv", "qn%d" % h, "sn%d" % h])
         store("y", T.oc[:, 4 * lo:4 * hi], T.qn[:, lo:hi].bitcast(dt.uint8), ["qn%d" % h])
-    act(T.ysb[:, 0:256], T.ps[:, 512 * banks[0]:512 * banks[0] + 256], ["ps%d" % banks[0]], ["y0"])
-    cp(T.ysb[:, 256:512], T.ps[:, 512 * banks[1]:512 * banks[1] + 256], ["ps%d" % banks[1]], ["y1"])
-    store("y", T.y[:, 0:256], T.ysb[:, 0:256], ["y0"])
-    store("y", T.y[:, 256:512], T.ysb[:, 256:512], ["y1"])
+        (cp if h else act)(T.ysb[:, lo:hi], T.ps[:, 512 * b:512 * b + 256], ["ps%d" % b, "sn1"], ["y%d" % h] , c=212)
+        store("y", T.y[:, lo:hi], T.ysb[:, lo:hi], ["y%d" % h])
     for k in range(4):
-        store("s", T.osc[4 * k:4 * k + 4, :], T.sn[32 * k:32 * k + 4, :], ["sn0", "sn1"])
+        store("s", T.osc[4 * k:4 * k + 4, :], T.sn[32 * k:32 * k + 4, :], ["sn0", "sn1", "y0"])
 
+    for i in schedule(nodes, ready):
+        nodes[i][4]()
     for s in sorted(count):
-        if count[s]:
-            g.wait_ge(T.sem[s], count[s])
+        g.wait_ge(T.sem[s], count[s])

@@ -4,11 +4,14 @@ F32, BF, I32, U16, U8, X4 = "float32", "bfloat16", "int32", "uint16", "uint8", "
 STEP = [1, 2, 3]
 SENT = -1.0e29
 JS = 152
-ORDER = ("L_0 Gb0 Ga0 Gb1 C0 QV0 Ga1 QV1 R_0 C1 L_1 X0 R_1 A_0 A_1 QT0 FD Gb2 Gc2 Gb3 QV2 SC0 QT1 SH0 R_2 Ga3 X1 SC1 QV3 R_3 X2 "
+ORDER = ("L_0 Gb0 Ga0 Gb1 C0 QV0 Ga1 QV1 R_0 C1 L_1 X0 R_1 A_0 A_1 QT0 FD Gb2 Ga2 Gb3 QV2 SC0 QT1 SH0 R_2 Gc3 X1 SC1 QV3 R_3 X2 "
          "A_2 A_3 QT2 QT3 SC2 SH1 SC3")
-WAKE, FAR, FARL, SLACK = 200, 4000, 2800, 40
+AFTER = "A_0>A_1 A_1>A_2 A_2>A_3 QT1>A_3"
+KEYV = (0,)
+WAKE, FAR, FARL, SLACK = 230, 4000, 2800, 40
 
-SCRATCH = {"ps": ("psum", [128, 4096], F32), "ptp": ("sbuf", [128, 5, 10], F32), "k0": ("sbuf", [128, 5, 11], F32)}
+SCRATCH = {"ps": ("psum", [128, 4096], F32), "ptp": ("sbuf", [128, 5, 10], F32), "k0": ("sbuf", [128, 5, 11], F32),
+           "r0": ("sbuf", [128, 4, 10], F32)}
 for _ty, _bufs in (
         (BF, dict(us=512, vs=512, ones=520, zt=520, dd=2048, tc0=2560, tc1=2560, tc2=2560, tc3=2560)),
         (X4, dict(qu=128, qv=128, qw=512, qe=512, qn=512, qz=512, qt0=512, qt1=512, qt2=512, qt3=512, lc0=512, lc1=512, lc2=512)),
@@ -17,7 +20,7 @@ for _ty, _bufs in (
         (U16, dict(lst=16, oa=32, ob=32, posl=32, off=128, oln=32, ll0=32, ll1=32, ll2=32, sl0=32, sl1=32, sl2=32)),
         (F32, dict(pf=64, pt=64, pf2=66, pt2=64, col=12, jb=6 * JS, d0=120, dk=150, ko=150, non=40, gg=60, yy=120, cd=120, cc=120,
                    e0=120, e1=120, rr=120, c01=40,
-                   lf=32, lft=32, in2=128, in2t=128, ln=32, lnt=32, ssb=512, kr=512, tp=512, a32=2048, olt=640, olr=512, ysb=512))):
+                   lf=32, lft=32, in2=128, in2t=128, ln=32, lnt=32, ssb=512, kr=512, tp=800, a32=2048, olt=640, olr=512, ysb=512))):
     for _k, _n in _bufs.items():
         SCRATCH[_k] = ("sbuf", [128, _n], _ty)
 
@@ -34,11 +37,11 @@ def schedule(nodes, ready):
         d = {}
         for k in list(nd[2]) + list(nd[3]):
             if k in wr:
-                d[wr[k]] = WAKE
+                d[wr[k]] = max(d.get(wr[k], 0), 0 if k[0] == "~" else WAKE)
             for j, lat in far.get(k, []):
                 d[j] = lat
         for k in nd[3]:
-            for j in rd.get(k, []):
+            for j in rd.get(k, []) if k[0] != "~" else []:
                 d[j] = WAKE
         d.pop(i, None)
         deps.append(d)
@@ -96,7 +99,8 @@ def rank_program(g, core, T, topo):
 
     def need(q, reads, writes):
         ev = {}
-        for k in list(reads) + list(writes):
+        reads, writes = [k for k in reads if k[0] != "~"], [k for k in writes if k[0] != "~"]
+        for k in reads + writes:
             if k in writer:
                 s, n = writer[k]
                 ev[s] = max(ev.get(s, 0), n)
@@ -228,6 +232,7 @@ def rank_program(g, core, T, topo):
     iota(T.iq[:], [[4, 32]], 0, 0, ["iq"])
     ms(T.k0[:], SENT, ["k0_0", "k0_1"])
     ms(T.ko[:], SENT, ["ko"])
+    ms(T.tp[:, 0:800:16], SENT, ["tp0", "tp1", "tp2", "tp3"])
     ms(T.d0[:], 0.0, ["right", "on"])
     ms(T.dk[:], 0.0, ["wn", "pk"])
     ms(T.e0[:], 0.0, ["ond", "nonr"])
@@ -335,20 +340,21 @@ def rank_program(g, core, T, topo):
         tc, nx = T["tc%d" % t], T["tc%d" % (t + 1)]
         tck = [k for m in range(4) for k in pk(t, m)]
         ok, okk = (T.oa, "oa") if t == 0 else (T.ob, "ob")
-        cp(T.kr[:, 0:128], T.ssb[:].indirect(ok[:, 0:8]), ssb_keys + [okk], ["kr0"], 215)
-        for i in range(1, 4):
-            act(T.kr[:, 128 * i:128 * i + 128], T.ssb[:].indirect(ok[:, 8 * i:8 * i + 8]), ssb_keys + [okk], ["kr%d" % i], c=230)
         for i in range(4):
-            tr(T.tp[:, 128 * i:128 * i + 128], T.kr[:, 128 * i:128 * i + 128], ["kr%d" % i], ["tp%d" % i], 106)
+            (cp if i in KEYV else act)(T.kr[:, 128 * i:128 * i + 128], T.ssb[:].indirect(ok[:, 8 * i:8 * i + 8]), ssb_keys + [okk], ["kr%d" % i], c=225)
+        for i in range(4):
+            tr(T.tp[:, 160 * i:160 * i + 128], T.kr[:, 128 * i:128 * i + 128], ["kr%d" % i], ["tp%d" % i], 106)
         for h in range(2):
-            cp(T.k0[:, 0:4, 5 * h:5 * h + 4], T.tp[:, 16 * h:512:32], ["tp0", "tp1", "tp2", "tp3"], ["k0_%d" % h])
+            tt(T.r0[:, 0, 5 * h:5 * h + 5], T.tp[:, 32 + 16 * h:192:32], T.tp[:, 160 + 16 * h:320:32], A.is_ge, ["tp0", "tp1"], ["ra%d" % h], 55)
+            tt(T.r0[:, 1:4, 5 * h:5 * h + 5], T.tp[:, 192 + 16 * h:672:32], T.tp[:, 320 + 16 * h:800:32], A.is_ge, ["tp1", "tp2", "tp3"], ["rb%d" % h], 55)
+            cp(T.k0[:, 0:4, 5 * h:5 * h + 5], T.tp[:, 16 * h:640:32], ["tp0", "tp1", "tp2", "tp3"], ["k0_%d" % h])
         for h in range(2):
             for b in range(4):
                 bk = mm(256, T.qe[:, 128 * b:128 * b + 128], T.se[:, 128 * b:128 * b + 128], T["lc%d" % t][:, 256 * h:256 * h + 256],
                         T["ls%d" % t][:, 256 * h:256 * h + 256], ["e%d" % b, "land%d_%d" % (t, h if t else 0)])
                 act(T.dd[:, 1024 * h + b:1024 * h + 1024:4], T.ps[:, 512 * bk:512 * bk + 256], ["ps%d" % bk, "kr3"], ["dd%d_%d" % (h, b)], c=212)
 
-        tt(T.d0[:, 1:120:3], T.k0[:, 0:4, 1:11], T.k0[:, 1:5, 0:10], A.is_ge, k0k, ["right"])
+        cp(T.d0[:, 1:120:3], T.r0[:], ["ra0", "ra1", "rb0", "rb1"], ["right"])
         for k in range(4):
             s = (0 if t == 0 else 1) if k == 0 else k + 1
             so = k + 2
@@ -358,9 +364,9 @@ def rank_program(g, core, T, topo):
                 kc, kr_, kd, n, kk = T.ko[:, 2:119:3], T.ko[:, 5:122:3], T.ko[:, 32:149:3], 39, ["ko"]
                 cp(T.d0[:, 1:117:3], T.rr[:, 2:117:3], ["rr"], ["right"])
             for i in range(3):
-                d = T.d0[:, 30 * i + 1:30 * i + 30:3] if k == 0 else T.rr[:, 30 * i + 2:30 * i + 30:3]
+                d = T.r0[:, i, :] if k == 0 else T.rr[:, 30 * i + 2:30 * i + 30:3]
                 scan(T.gg[:, 10 * i + 10:10 * i + 20], d, T.gg[:, 10 * i:10 * i + 10], 1.0, A.mult, A.max,
-                     ["right" if k == 0 else "rr", "gc", "gc2"] + gk[max(i - 1, 0):i], ["g%d" % i], 55)
+                     (["rr"] if k else ["rb0", "rb1"] if i else ["ra0", "ra1"]) + ["gc", "gc2"] + gk[max(i - 1, 0):i], ["g%d" % i], 55)
             if k < 3:
                 tt(T.dk[:, 1:3 * n:3], kr_, kd, A.max, kk, ["wn"])
                 tt(T.e1[:, 2:3 * n:3], T.dk[:, 4:3 * n + 3:3], kd, A.is_ge, kk + ["wn"], ["c10"])
@@ -395,6 +401,7 @@ def rank_program(g, core, T, topo):
         bk, sk = {}, {}
         for name in ORDER.split():
             k, m = name[0:2], int(name[2:] or 0)
+            first = len(nodes)
             ak = ["a%d_%d" % (m, b) for b in range(4)]
             piece = nx[:, 512 * m:512 * m + 512]
             if k == "L_":
@@ -448,6 +455,9 @@ def rank_program(g, core, T, topo):
             elif k == "X2" and t == 2:
                 act(T.olr[:], T.olt[:].indirect(T.oln[:]), ["oln", "a3_3"] + ["olt%d" % i for i in range(5)], ["olr"], c=730)
                 store("y", T.ol[:], T.olr[0:128:16, :], ["olr"])
+            if len(nodes) > first:
+                nodes[first][2].extend("~%d%s" % (t, e[0:3]) for e in AFTER.split() if e[4:] == name)
+                nodes[first if k in ("QT", "QV") else -1][3].append("~%d%s" % (t, name))
 
     for t in range(3):
         one_round(t)
@@ -457,9 +467,11 @@ def rank_program(g, core, T, topo):
         lo, hi = 256 * h, 256 * h + 256
         cp(T.qn[:, lo:hi].bitcast(dt.uint32), T.qt3[:, 0:512].bitcast(dt.uint32).indirect(T.posl[:, 16 * h:16 * h + 16]), qk, ["qn%d" % h], 390)
         act(T.sn[:, lo:hi], T.st3[:, 0:512].indirect(T.posl[:, 16 * h:16 * h + 16]), qk, ["sn%d" % h], c=390)
+    for h in range(2):
+        lo, hi = 256 * h, 256 * h + 256
         b = mm(256, T.qv[:], T.sv[:], T.qn[:, lo:hi], T.sn[:, lo:hi], ["qv", "qn%d" % h, "sn%d" % h])
         store("y", T.oc[:, 4 * lo:4 * hi], T.qn[:, lo:hi].bitcast(dt.uint8), ["qn%d" % h])
-        (cp if h else act)(T.ysb[:, lo:hi], T.ps[:, 512 * b:512 * b + 256], ["ps%d" % b, "sn1"], ["y%d" % h] , c=212)
+        (cp if h else act)(T.ysb[:, lo:hi], T.ps[:, 512 * b:512 * b + 256], ["ps%d" % b, "sn1"], ["y%d" % h], c=212)
         store("y", T.y[:, lo:hi], T.ysb[:, lo:hi], ["y%d" % h])
     for k in range(4):
         store("s", T.osc[4 * k:4 * k + 4, :], T.sn[32 * k:32 * k + 4, :], ["sn0", "sn1", "y0"])

from concourse.mybir import dt, AluOpType as A, ActivationFunctionType as AF

F32, BF, I32, U16, U8, X4 = "float32", "bfloat16", "int32", "uint16", "uint8", "float8_e4m3fn_x4"
STEP = [1, 2, 3]
SENT = -1.0e29
JS = 152
ORDER = ("L_0 Gb0 Ga0 Gb1 C0 QV0 Ga1 QV1 R_0 C1 L_1 X0 R_1 A_0 A_1 QT0 FD Gb2 Ga2 Gb3 QV2 SC0 QT1 SH0 R_2 Gc3 X1 SC1 QV3 R_3 X2 "
         "A_2 A_3 QT2 QT3 SC2 SH1 SC3")
AFTER = "A_0>A_1 A_1>A_2 A_2>A_3 QT1>A_3"
KEYV = (0,)
WAKE, FAR, FARL, SLACK = 230, 4000, 2800, 40

SCRATCH = {"ps": ("psum", [128, 4096], F32), "ptp": ("sbuf", [128, 5, 10], F32), "k0": ("sbuf", [128, 5, 11], F32),
           "r0": ("sbuf", [128, 4, 10], F32)}
for _ty, _bufs in (
        (BF, dict(us=512, vs=512, ones=520, zt=520, dd=2048, tc0=2560, tc1=2560, tc2=2560, tc3=2560)),
        (X4, dict(qu=128, qv=128, qw=512, qe=512, qn=512, qz=512, qt0=512, qt1=512, qt2=512, qt3=512, lc0=512, lc1=512, lc2=512)),
        (U8, dict(su=128, sv=128, sw=512, se=512, sn=512, sz=512, st0=512, st1=512, st2=512, st3=512, ls0=512, ls1=512, ls2=512)),
        (I32, dict(pi=68, w1=66, w2=66, w3=66, w4=66, w5=66, ip=4, cb=4, iq=32, sm=40)),
        (U16, dict(lst=16, oa=32, ob=32, posl=32, off=128, oln=32, ll0=32, ll1=32, ll2=32, sl0=32, sl1=32, sl2=32)),
        (F32, dict(pf=64, pt=64, pf2=66, pt2=64, col=12, jb=6 * JS, d0=120, dk=150, ko=150, non=40, gg=60, yy=120, cd=120, cc=120,
                   e0=120, e1=120, rr=120, c01=40,
                   lf=32, lft=32, in2=128, in2t=128, ln=32, lnt=32, ssb=512, kr=512, tp=800, a32=2048, olt=640, olr=512, ysb=512))):
    for _k, _n in _bufs.items():
        SCRATCH[_k] = ("sbuf", [128, _n], _ty)

SEMAPHORES = ["cv", "cs", "cp", "cg", "x0", "x1", "x2", "x3", "lu", "lp", "lw", "lv", "snd", "outs"] + \
    ["ar%d_%d" % (t, h) for t in range(3) for h in range(2)] + ["al%d" % t for t in range(3)]


def schedule(nodes, ready):
    deps, wr, rd, far = [], {}, {}, {}
    for i, nd in enumerate(nodes):
        if nd[5]:
            far.setdefault(nd[5][0], []).append((i, nd[5][1]))
    for i, nd in enumerate(nodes):
        d = {}
        for k in list(nd[2]) + list(nd[3]):
            if k in wr:
                d[wr[k]] = max(d.get(wr[k], 0), 0 if k[0] == "~" else WAKE)
            for j, lat in far.get(k, []):
                d[j] = lat
        for k in nd[3]:
            for j in rd.get(k, []) if k[0] != "~" else []:
                d[j] = WAKE
        d.pop(i, None)
        deps.append(d)
        for k in nd[2]:
            rd.setdefault(k, []).append(i)
        for k in nd[3]:
            wr[k] = i
            rd[k] = []
    n = len(nodes)
    succ = [[] for _ in range(n)]
    for i in range(n):
        for j in deps[i]:
            succ[j].append(i)
    pri = [0.0] * n
    for i in range(n - 1, -1, -1):
        pri[i] = nodes[i][1] + max([deps[j][i] + pri[j] for j in succ[i]] + [0])
    left = [len(d) for d in deps]
    cand = [i for i in range(n) if not left[i]]
    end, free, order = [0.0] * n, {}, []

    def start(i):
        return max([free.get(nodes[i][0], 0.0)] + [end[j] + lat for j, lat in deps[i].items()] + [ready.get(k, 0) for k in nodes[i][2]])

    while cand:
        best = None
        for q in sorted(set(nodes[i][0] for i in cand)):
            c = sorted((i for i in cand if nodes[i][0] == q), key=lambda i: (-pri[i], i))
            pick, limit = c[0], start(c[0])
            for i in c[1:]:
                if start(i) + nodes[i][1] <= limit + SLACK and start(i) < start(pick):
                    pick, limit = i, min(limit, start(i) + nodes[i][1])
            if best is None or start(pick) < best[0]:
                best = (start(pick), pick)
        st, i = best
        end[i] = free[nodes[i][0]] = st + nodes[i][1]
        order.append(i)
        cand.remove(i)
        for j in succ[i]:
            left[j] -= 1
            if not left[j]:
                cand.append(j)
    return order


def rank_program(g, core, T, topo):
    rank = T.rank_of(core)
    if rank is None:
        return
    N = len(T.cores)
    Q = {"v": g.vector, "s": g.scalar, "p": g.tensor, "g": g, "y": g.sync}
    CSEM = {"v": "cv", "s": "cs", "p": "cp", "g": "cg"}
    count = {"cv": 0, "cs": 0, "cp": 0, "cg": 0, "snd": 0, "outs": 0}
    waited = {q: {} for q in Q}
    writer, readers, nodes, ready = {}, {}, [], {}

    def need(q, reads, writes):
        ev = {}
        reads, writes = [k for k in reads if k[0] != "~"], [k for k in writes if k[0] != "~"]
        for k in reads + writes:
            if k in writer:
                s, n = writer[k]
                ev[s] = max(ev.get(s, 0), n)
        for k in writes:
            for s, n in readers.get(k, {}).items():
                ev[s] = max(ev.get(s, 0), n)
        for s in sorted(ev):
            if waited[q].get(s, 0) < ev[s]:
                Q[q].wait_ge(T.sem[s], ev[s])
                waited[q][s] = ev[s]

    def note(ev, reads, writes):
        for k in reads:
            d = readers.setdefault(k, {})
            d[ev[0]] = max(d.get(ev[0], 0), ev[1])
        for k in writes:
            writer[k] = ev
            readers[k] = {}

    def op(q, fn, reads, writes, cost):
        def issue():
            need(q, reads, writes)
            s = CSEM[q]
            fn().then_inc(T.sem[s], 1)
            count[s] += 1
            note((s, count[s]), reads, writes)
        nodes.append((q, cost, reads, writes, issue, None))

    def load(q, sem, total, out, in_, writes, at):
        Q[q].dma_start(out, in_).then_inc(T.sem[sem], 16)
        note((sem, total), [], writes)
        for k in writes:
            ready[k] = at

    def store(q, out, in_, reads):
        def issue():
            need(q, reads, [])
            Q[q].dma_start(out, in_).then_inc(T.sem.outs, 16)
            count["outs"] += 16
        nodes.append((q, 60, reads, [], issue, None))

    V = g.vector

    def tt(o, a, b, o_, r, w, c=65):
        op("v", lambda: V.tensor_tensor(o, a, b, o_), r, w, c)

    def ts(o, a, s1, s2, o0, o1, r, w):
        if o1 is None:
            op("v", lambda: V.tensor_scalar(o, a, s1, None, o0), r, w, 55)
        else:
            op("v", lambda: V.tensor_scalar(o, a, s1, s2, o0, o1), r, w, 55)

    def cp(o, a, r, w, c=55):
        op("v", lambda: V.tensor_copy(o, a), r, w, c)

    def tr(o, a, r, w, c=55):
        op("v", lambda: V.transpose(o, a), r, w, c)

    def ms(o, c, w):
        op("v", lambda: V.memset(o, c), [], w, 90)

    def scan(o, a, b, init, o0, o1, r, w, c=100):
        op("v", lambda: V.tensor_tensor_scan(o, a, b, init, o0, o1), r, w, c)

    def quant(q, s, a, r, w):
        op("v", lambda: V.quantize_mx(q, s, a), r, w, 125)

    def act(o, a, r, w, func=AF.Copy, c=106, **kw):
        op("s", lambda: g.scalar.activation(o, a, func, **kw), r, w, c)

    def iota(o, pat, base, cm, w, flt=False):
        if flt:
            op("g", lambda: g.iota(o, pat, base, cm, allow_small_or_imprecise_dtypes=True), ["sent0"], w, 340)
        else:
            op("g", lambda: g.iota(o, pat, base, cm), [], w, 140)

    bank = [0]

    def mm(n, lq, lsc, rq, rsc, r):
        b = bank[0] % 8
        bank[0] += 1
        op("p", lambda: g.tensor.matmul_mx(T.ps[:, 512 * b:512 * b + n], lq, lsc, rq, rsc, True, True), r, ["ps%d" % b], 0.6 * n + 10)
        return b

    def send(t, out, in_, sem, reads, key, lat, w=()):
        def issue():
            dst = T.cores[(rank + STEP[t]) % N]
            rid, pid = topo.addr(dst)[0:2]
            need("g", reads, [])
            g.remote_dma(out, in_, T.sem[sem], T.sem.snd, pid, rid, topo.mask(core, dst))
            count["snd"] += len(topo.engines(core, dst))
        nodes.append(("g", 500, reads, ["sends"] + list(w), issue, (key, lat)))

    def arriving(t):
        return len(topo.engines(T.cores[(rank - STEP[t]) % N], core))

    for t in range(3):
        for h in range(2):
            writer["land%d_%d" % (t, h)] = ("ar%d_%d" % (t, h), 2 * arriving(t))
        writer["ll%d" % t] = ("al%d" % t, arriving(t))
    writer["land0_0"] = ("ar0_0", 3 * arriving(0))

    def send_codes(t, m0, m1, h):
        send(t, T["lc%d" % t][:, 128 * m0:128 * m1].bitcast(dt.uint8), T["qt%d" % t][:, 128 * m0:128 * m1].bitcast(dt.uint8), "ar%d_%d" % (t, h),
             ["qt%d_%d" % (t, m) for m in range(m0, m1)], "land%d_%d" % (t, h), FAR)

    def send_scales(t, m0, m1, h):
        send(t, T["ls%d" % t][:, 128 * m0:128 * m1], T["st%d" % t][:, 128 * m0:128 * m1], "ar%d_%d" % (t, h),
             ["qt%d_%d" % (t, m) for m in range(m0, m1)], "land%d_%d" % (t, h), FAR)

    def pk(t, m):
        return ["tc%d_%d_0" % (t, m), "tc%d_%d_1" % (t, m)]

    for m in range(4):
        load("y", "x%d" % m, 16, T.tc0[:, 512 * m:512 * m + 512], T.x[:, 512 * m:512 * m + 512], pk(0, m), 2500 + 400 * m)
    load("s", "lu", 16, T.us[:], T.u[:], ["us"], 2300)
    load("s", "lp", 144, T.pi[:, 0:32], T.p[:], ["pi"], 3500)
    for a in range(4):
        for h in range(2):
            load("s", "lp", 144, T.pi[32 * a:32 * a + 32, 32 + 16 * h:48 + 16 * h], T.p[32 * a + 16 * h:32 * a + 16 * h + 16, :], ["pi"], 3500)
    load("s", "lw", 32, T.qw[:].bitcast(dt.uint8), T.wc[:], ["w"], 5000)
    load("s", "lw", 32, T.sw[:], T.ws[:], ["w"], 5000)
    load("s", "lv", 16, T.vs[:], T.v[:], ["vs"], 20000)

    iota(T.ip[:], [[0, 4]], 0, 1, ["ip"])
    iota(T.cb[:], [[4, 4]], 0, 0, ["cb"])
    ms(T.ones[:], 1.0, ["ones"])
    op("g", lambda: g.affine_select(T.zt[:], T.ones[:], [[-1, 520]], A.is_equal, 0.0, 3, 4), ["ones", "ip", "cb"], ["zt"], 1030)
    iota(T.iq[:], [[4, 32]], 0, 0, ["iq"])
    ms(T.k0[:], SENT, ["k0_0", "k0_1"])
    ms(T.ko[:], SENT, ["ko"])
    ms(T.tp[:, 0:800:16], SENT, ["tp0", "tp1", "tp2", "tp3"])
    ms(T.d0[:], 0.0, ["right", "on"])
    ms(T.dk[:], 0.0, ["wn", "pk"])
    ms(T.e0[:], 0.0, ["ond", "nonr"])
    ms(T.gg[:], 1.0, ["g0", "g1", "g2", "gc", "gc2"])
    ms(T.cd[:], -1.0e9, ["cd"])
    ms(T.dk[:, 118:150:3], SENT, ["wn"])
    ms(T.gg[:, 0:4], 0.0, ["gc"])
    ms(T.gg[:, 5:9], 0.0, ["gc2"])
    ms(T.cd[:, 0:120:3], 1.0e9, ["cd"])
    sm, col = T.sm, T.col
    ts(sm[:, 16:20], T.ip[:], 31, None, A.bitwise_and, None, ["ip"], ["sj"])
    ts(sm[:, 0:4], T.ip[:], 2, 3, A.arith_shift_right, A.bitwise_and, ["ip"], ["sr"])
    ts(sm[:, 20:21], T.ip[:, 0:1], 3, None, A.bitwise_and, None, ["ip"], ["st"])
    ts(col[:, 1:2], sm[:, 16:17], 16.0, 2060.0, A.mult, A.add, ["sj"], ["m3"])
    ts(col[:, 4:8], sm[:, 16:20], 48.0, 6168.0, A.mult, A.add, ["sj"], ["yb0"])
    tt(sm[:, 4:8], sm[:, 0:4], T.cb[:], A.add, ["sr", "cb"], ["sm"])
    cp(col[:, 0:1], sm[:, 20:21], ["st"], ["tcol"])
    jk = lambda z: ["j%d" % z, "t%d" % z, "u%d" % z]
    act(T.jb[:, 0:3 * JS], T.ones[:, 0:3 * JS], ["ones", "m3"], jk(0) + jk(1) + jk(2), AF.Identity, 380, bias=col[:, 1:2], scale=0.0)
    act(T.ptp[:], T.ones[:, 0:50], ["ones", "m3"], ["ptp0", "ptp1"], AF.Identity, 55, bias=col[:, 1:2], scale=0.0)
    act(T.jb[:, 3 * JS:6 * JS], T.ones[:, 0:3 * JS], ["ones", "m3"], jk(3) + jk(4) + jk(5), AF.Identity, 380, bias=col[:, 1:2], scale=0.0)
    ts(sm[:, 21:22], sm[:, 0:1], 10.0, None, A.mult, None, ["sr"], ["s10"])
    ts(sm[:, 24:25], sm[:, 0:1], 1.0, None, A.min, None, ["sr"], ["smin"])
    ts(sm[:, 8:12], sm[:, 4:8], 43.0, None, A.mult, None, ["sm"], ["si"])
    tt(col[:, 8:12], col[:, 4:8], T.cb[:], A.add, ["yb0", "cb"], ["yb"])
    tt(sm[:, 22:23], sm[:, 0:1], sm[:, 24:25], A.add, ["sr", "smin"], ["ska"])
    ts(sm[:, 28:32], sm[:, 8:12], 7, None, A.arith_shift_right, None, ["si"], ["si2"])
    tt(sm[:, 23:24], sm[:, 21:22], sm[:, 20:21], A.add, ["s10", "st"], ["snat"])
    ts(sm[:, 15:16], sm[:, 21:22], 3.0, None, A.add, None, ["s10"], ["sx3"])
    ts(sm[:, 32:36], sm[:, 28:32], 7.0, None, A.mult, None, ["si2"], ["si3"])
    for h in range(2):
        ts(T.lst[:, 8 + h:9 + h], sm[:, 22:23], float(JS), 2.0 + 15 * h, A.mult, A.add, ["ska"], ["lfa%d" % h])
        ts(T.lst[:, 10 + h:11 + h], sm[:, 0:1], float(JS), JS + 2.0 + 15 * h, A.mult, A.add, ["sr"], ["lfb%d" % h])
        ts(T.lst[:, 12 + h:13 + h], sm[:, 23:24], 3.0, 2.0 + 15 * h, A.mult, A.add, ["snat"], ["lnl%d" % h])
    tt(sm[:, 12:15], sm[:, 4:7], sm[:, 32:35], A.add, ["sm", "si3"], ["sx"])
    ts(T.pi[:, 64:66], T.ip[:, 0:2], 15, None, A.bitwise_and, None, ["ip"], ["pi2"])
    for h in range(2):
        ts(T.lst[:, h:8:2], sm[:, 12:16], 3.0, 2.0 + 15 * h, A.mult, A.add, ["sx", "sx3"], ["la%d" % h])

    def tu(s):
        o = s * JS
        tt(T.jb[:, o:o + 117:3], T.jb[:, o + 5:o + 122:3], T.jb[:, o + 32:o + 149:3], A.subtract, ["j%d" % s], ["t%d" % s])

    def uu(s):
        o = s * JS
        tt(T.jb[:, o + 1:o + 118:3], T.jb[:, o + 32:o + 149:3], T.jb[:, o + 2:o + 119:3], A.subtract, ["j%d" % s], ["u%d" % s])

    def first_ids(s, pt, key):
        ts(T.ptp[:, 0:4, 0:4], pt[:, 0:16], 4.0, None, A.mult, None, [key], ["ptp0"])
        ts(T.ptp[:, 0:4, 5:9], pt[:, 16:32], 4.0, None, A.mult, None, [key], ["ptp1"])
        cp(T.jb[:, s * JS + 2:s * JS + 150:3], T.ptp[:], ["ptp0", "ptp1"], ["j%d" % s])
        tu(s)
        uu(s)

    def key_piece(t, m):
        return mm(128, T.qu[:], T.su[:], T["qt%d" % t][:, 128 * m:128 * m + 128], T["st%d" % t][:, 128 * m:128 * m + 128], ["qu", "qt%d_%d" % (t, m)])

    def key_copy(m, b):
        act(T.ssb[:, 128 * m:128 * m + 128], T.ps[:, 512 * b:512 * b + 128], ["ps%d" % b], ["ssb%d" % m])

    def qt_piece(t, m):
        quant(T["qt%d" % t][:, 128 * m:128 * m + 128], T["st%d" % t][:, 128 * m:128 * m + 128], T["tc%d" % t][:, 512 * m:512 * m + 512],
              pk(t, m), ["qt%d_%d" % (t, m)])

    for b in range(4):
        quant(T.qe[:, 128 * b:128 * b + 128], T.se[:, 128 * b:128 * b + 128], T.zt[:, 3 - b:515 - b], ["zt"], ["e%d" % b])
    quant(T.qu[:], T.su[:], T.us[:], ["us"], ["qu"])
    quant(T.qv[:], T.sv[:], T.vs[:], ["vs"], ["qv"])
    for m in range(4):
        qt_piece(0, m)
        key_copy(m, key_piece(0, m))
    send_codes(0, 0, 1, 0)
    send_codes(0, 1, 4, 0)
    send_scales(0, 0, 4, 0)
    cp(T.pf[:], T.pi[:, 0:64], ["pi"], ["pf"])
    tr(T.pt[:], T.pf[:], ["pf"], ["pt"])
    cp(T.oa[:], T.pt[:, 32:64], ["pt"], ["oa"])
    first_ids(0, T.pt, "pt")

    def positions():
        pi, r = T.pi[:, 0:66], ["pi", "pi2", "oa"]
        ts(T.w1[:], pi, 3, None, A.bitwise_and, None, r, ["w1"])
        ts(T.w2[:], pi, 2, 3, A.arith_shift_right, A.bitwise_and, r, ["w2"])
        ts(T.w3[:], pi, 2, 124, A.arith_shift_right, A.bitwise_and, r, ["w3"])
        ts(T.w4[:], T.w1[:], 3.0, None, A.is_equal, None, ["w1"], ["w4"])
        ts(T.w5[:], T.w2[:], -2.0, 9.0, A.mult, A.add, ["w2"], ["w5"])
        ts(T.w2[:], T.w2[:], 3.0, None, A.mult, None, ["w2"], ["w2"])
        tt(T.w4[:], T.w4[:], T.w5[:], A.mult, ["w4", "w5"], ["w4"], 110)
        tt(T.w1[:], T.w1[:], T.w2[:], A.add, ["w1", "w2"], ["w1"], 110)
        tt(T.w1[:], T.w1[:], T.w4[:], A.add, ["w1", "w4"], ["w1"], 110)
        ts(T.w2[:], T.w1[:], 2, None, A.arith_shift_right, None, ["w1"], ["w2"])
        tt(T.w3[:], T.w3[:], T.w1[:], A.add, ["w1", "w3"], ["w3"], 110)
        ts(T.w2[:], T.w2[:], 124.0, None, A.mult, None, ["w2"], ["w2"])
        tt(T.pf2[:], T.w3[:], T.w2[:], A.add, ["w2", "w3"], ["pf2"], 110)
        tr(T.pt2[:], T.pf2[:, 0:64], ["pf2"], ["pt2"])
        ts(T.posl[:], T.iq[:], T.pf2[:, 64:65], None, A.add, None, ["pf2", "iq"], ["posl"])
        cp(T.ob[:], T.pt2[:, 32:64], ["pt2"], ["ob"])
        first_ids(1, T.pt2, "pt2")

    ssb_keys = ["ssb%d" % m for m in range(4)]
    gk = ["g0", "g1", "g2"]
    k0k = ["k0_0", "k0_1"]

    def one_round(t):
        tc, nx = T["tc%d" % t], T["tc%d" % (t + 1)]
        tck = [k for m in range(4) for k in pk(t, m)]
        ok, okk = (T.oa, "oa") if t == 0 else (T.ob, "ob")
        for i in range(4):
            (cp if i in KEYV else act)(T.kr[:, 128 * i:128 * i + 128], T.ssb[:].indirect(ok[:, 8 * i:8 * i + 8]), ssb_keys + [okk], ["kr%d" % i], c=225)
        for i in range(4):
            tr(T.tp[:, 160 * i:160 * i + 128], T.kr[:, 128 * i:128 * i + 128], ["kr%d" % i], ["tp%d" % i], 106)
        for h in range(2):
            tt(T.r0[:, 0, 5 * h:5 * h + 5], T.tp[:, 32 + 16 * h:192:32], T.tp[:, 160 + 16 * h:320:32], A.is_ge, ["tp0", "tp1"], ["ra%d" % h], 55)
            tt(T.r0[:, 1:4, 5 * h:5 * h + 5], T.tp[:, 192 + 16 * h:672:32], T.tp[:, 320 + 16 * h:800:32], A.is_ge, ["tp1", "tp2", "tp3"], ["rb%d" % h], 55)
            cp(T.k0[:, 0:4, 5 * h:5 * h + 5], T.tp[:, 16 * h:640:32], ["tp0", "tp1", "tp2", "tp3"], ["k0_%d" % h])
        for h in range(2):
            for b in range(4):
                bk = mm(256, T.qe[:, 128 * b:128 * b + 128], T.se[:, 128 * b:128 * b + 128], T["lc%d" % t][:, 256 * h:256 * h + 256],
                        T["ls%d" % t][:, 256 * h:256 * h + 256], ["e%d" % b, "land%d_%d" % (t, h if t else 0)])
                act(T.dd[:, 1024 * h + b:1024 * h + 1024:4], T.ps[:, 512 * bk:512 * bk + 256], ["ps%d" % bk, "kr3"], ["dd%d_%d" % (h, b)], c=212)

        cp(T.d0[:, 1:120:3], T.r0[:], ["ra0", "ra1", "rb0", "rb1"], ["right"])
        for k in range(4):
            s = (0 if t == 0 else 1) if k == 0 else k + 1
            so = k + 2
            if k == 0:
                kc, kr_, kd, n, kk = T.k0[:, 0:4, 0:10], T.k0[:, 0:4, 1:11], T.k0[:, 1:5, 0:10], 40, k0k
            else:
                kc, kr_, kd, n, kk = T.ko[:, 2:119:3], T.ko[:, 5:122:3], T.ko[:, 32:149:3], 39, ["ko"]
                cp(T.d0[:, 1:117:3], T.rr[:, 2:117:3], ["rr"], ["right"])
            for i in range(3):
                d = T.r0[:, i, :] if k == 0 else T.rr[:, 30 * i + 2:30 * i + 30:3]
                scan(T.gg[:, 10 * i + 10:10 * i + 20], d, T.gg[:, 10 * i:10 * i + 10], 1.0, A.mult, A.max,
                     (["rr"] if k else ["rb0", "rb1"] if i else ["ra0", "ra1"]) + ["gc", "gc2"] + gk[max(i - 1, 0):i], ["g%d" % i], 55)
            if k < 3:
                tt(T.dk[:, 1:3 * n:3], kr_, kd, A.max, kk, ["wn"])
                tt(T.e1[:, 2:3 * n:3], T.dk[:, 4:3 * n + 3:3], kd, A.is_ge, kk + ["wn"], ["c10"])
                tt(T.c01[:, 0:n], kr_, T.dk[:, 31:3 * n + 30:3], A.is_ge, kk + ["wn"], ["c01"])
                tt(T.e1[:, 1:3 * n:3], T.d0[:, 1:3 * n:3], T.e1[:, 2:3 * n:3], A.subtract, ["right", "c10"], ["ed"])
                tt(T.e1[:, 0:3 * n:3], T.c01[:, 0:n], T.d0[:, 1:3 * n:3], A.subtract, ["right", "c01"], ["eb"])
            if k == 2:
                scan(T.jb[:, 4 * JS:4 * JS + 18], T.d0[:, 0:18], T.jb[:, 3 * JS:3 * JS + 18], 0.0, A.mult, A.add, ["right", "on"] + jk(3), jk(4), 55)
                c0 = 8 if t == 0 else 10
                cp(T.lf[:], T.jb[:, 0:5 * JS].indirect(T.lst[:, c0:c0 + 2]), [x for z in range(5) for x in jk(z)] + ["lfa0", "lfa1", "lfb0", "lfb1"], ["lf"], 92)
                tr(T.lft[:], T.lf[:], ["lf"], ["lft"])
                ts(T["sl%d" % t][:], T.lft[:], col[:, 0:1], None, A.add, None, ["lft", "tcol"], ["sl%d" % t])
                send(t, T["ll%d" % t][:], T["sl%d" % t][:], "al%d" % t, ["sl%d" % t], "ll%d" % t, FARL, ["sent0"] if t == 0 else [])
            if k < 3:
                tt(T.e0[:, 1:117:3], T.gg[:, 19:58], T.gg[:, 10:49], A.is_gt, gk, ["ond"])
                tt(T.e0[:, 2:117:3], T.gg[:, 10:49], T.gg[:, 1:40], A.is_le, gk, ["nonr"])
                scan(T.rr[:, 0:117], T.e0[:, 0:117], T.e1[:, 0:117], 0.0, A.mult, A.add, ["ond", "nonr", "c10", "ed", "eb"], ["rr"])
            tt(T.d0[:, 2:117:3], T.gg[:, 9:48], T.gg[:, 0:39], A.is_gt, gk, ["on"])
            if k < 2:
                tt(T.non[:, 0:n], T.gg[:, 9:9 + n], T.gg[:, 0:n], A.is_le, gk, ["non"])
                tt(T.dk[:, 2:3 * n:3], T.non[:, 0:n], kc, A.mult, kk + ["non"], ["pk"])
                scan(T.ko[:, 0:117], T.d0[:, 0:117], T.dk[:, 0:117], 0.0, A.mult, A.add, ["right", "on", "wn", "pk"], ["ko"])
            scan(T.jb[:, so * JS:so * JS + 117], T.d0[:, 0:117], T.jb[:, s * JS:s * JS + 117], 0.0, A.mult, A.add, ["right", "on"] + jk(s), jk(so))
            if k < 3:
                tu(so)
                uu(so)
                act(T.yy[:, k:117:3], T.jb[:, so * JS + 2:so * JS + 119:3], jk(so) + ["yb"], ["yy%d" % k], AF.Identity, 55, bias=col[:, 8 + k:9 + k], scale=-2.0)
        if t == 0:
            positions()

        win = T.jb[:, 5 * JS:6 * JS]
        bk, sk = {}, {}
        for name in ORDER.split():
            k, m = name[0:2], int(name[2:] or 0)
            first = len(nodes)
            ak = ["a%d_%d" % (m, b) for b in range(4)]
            piece = nx[:, 512 * m:512 * m + 512]
            if k == "L_":
                c = slice(64 * m, 64 * m + 64)
                cp(T.in2[:, c], win.indirect(T.lst[:, 4 * m:4 * m + 4]), jk(5) + ["la0", "la1"], ["in2_%d" % m], 133)
                tr(T.in2t[:, c], T.in2[:, c], ["in2_%d" % m], ["in2t%d" % m])
                ts(T.off[:, c], T.in2t[:, c], col[:, 0:1], None, A.add, None, ["in2t%d" % m, "tcol"], ["off%d" % m])
            elif k[0] == "G":
                q, hf = {"Ga": (cp, 0), "Gb": (act, 1), "Gc": (act, 0), "Gd": (cp, 1)}[k]
                w = tc[:, 0:2048] if m < 2 else tc[:, 0:2560]
                q(nx[:, 512 * m + 256 * hf:512 * m + 256 * hf + 256], w.indirect(T.off[:, 32 * m + 16 * hf:32 * m + 16 * hf + 16]),
                  tck + ["off%d" % (m // 2)] + ([] if m < 2 else ["fd%d" % t]), pk(t + 1, m)[hf:hf + 1], c=390)
            elif k == "QV":
                c = slice(128 * m, 128 * m + 128)
                quant(T.qz[:, c], T.sz[:, c], piece, pk(t + 1, m), ["qz%d" % m])
                bk[m] = [mm(128, T.qw[:, 128 * b:128 * b + 128], T.sw[:, 128 * b:128 * b + 128], T.qz[:, c], T.sz[:, c], ["w", "qz%d" % m]) for b in range(4)]
            elif k == "R_":
                for b in range(4):
                    act(T.a32[:, 512 * m + b:512 * m + 512:4], T.ps[:, 512 * bk[m][b]:512 * bk[m][b] + 128], ["ps%d" % bk[m][b]], [ak[b]],
                        AF.Relu, scale=0.015625)
            elif k == "A_":
                tt(piece, T.a32[:, 512 * m:512 * m + 512], piece, A.add, ak + pk(t + 1, m), pk(t + 1, m), 850)
            elif k == "QT":
                qt_piece(t + 1, m)
                if t < 2:
                    sk[m] = key_piece(t + 1, m)
            elif k == "SC" and t < 2:
                key_copy(m, sk[m])
            elif k == "SH" and t < 2:
                send_codes(t + 1, 2 * m, 2 * m + 2, m)
                send_scales(t + 1, 2 * m, 2 * m + 2, m)
            elif k == "C0":
                scan(T.cc[:, 0:117], T.cd[:, 0:117], T.yy[:, 0:117], 0.0, A.max, A.min, ["cd", "yy0", "yy1", "yy2"], ["cc"])
            elif k == "C1":
                tt(T.jb[:, 5 * JS + 2:5 * JS + 119:3], T.jb[:, 5 * JS + 2:5 * JS + 119:3], T.cc[:, 2:117:3], A.min, ["j5", "cc"], ["j5"])
            elif k == "FD":
                act(tc[:, 2048:2560], T.dd[:].indirect(T["ll%d" % t][:]), ["dd%d_%d" % (h, b) for h in range(2) for b in range(4)] + ["ll%d" % t],
                    ["fd%d" % t], c=730)
            elif k == "X0" and t == 0:
                iota(T.olt[:, 0:128], [[16, 32], [1, 4]], 0, 0, ["olt0"], True)
                iota(T.olt[:, 256:384], [[16, 32], [1, 4]], 11, 0, ["olt2"], True)
                iota(T.olt[:, 128:256], [[16, 32], [3, 2], [1, 2]], 5, 0, ["olt1"], True)
                iota(T.olt[:, 3:128:4], [[16, 32]], 4, 0, ["olt0"], True)
                iota(T.olt[:, 256:384:4], [[16, 32]], 10, 0, ["olt2"], True)
                iota(T.olt[:, 384:512], [[16, 32], [4, 4]], 3, 0, ["olt3"], True)
                iota(T.olt[:, 512:640], [[1, 32], [32, 4]], 512, 0, ["olt4"], True)
            elif k == "X1" and t == 2:
                cp(T.ln[:], win.indirect(T.lst[:, 12:14]), jk(5) + ["lnl0", "lnl1"], ["ln"], 92)
                tr(T.lnt[:], T.ln[:], ["ln"], ["lnt"])
                ts(T.oln[:], T.lnt[:], 0.25, None, A.mult, None, ["lnt"], ["oln"])
            elif k == "X2" and t == 2:
                act(T.olr[:], T.olt[:].indirect(T.oln[:]), ["oln", "a3_3"] + ["olt%d" % i for i in range(5)], ["olr"], c=730)
                store("y", T.ol[:], T.olr[0:128:16, :], ["olr"])
            if len(nodes) > first:
                nodes[first][2].extend("~%d%s" % (t, e[0:3]) for e in AFTER.split() if e[4:] == name)
                nodes[first if k in ("QT", "QV") else -1][3].append("~%d%s" % (t, name))

    for t in range(3):
        one_round(t)

    qk = ["qt3_%d" % m for m in range(4)] + ["posl"]
    for h in range(2):
        lo, hi = 256 * h, 256 * h + 256
        cp(T.qn[:, lo:hi].bitcast(dt.uint32), T.qt3[:, 0:512].bitcast(dt.uint32).indirect(T.posl[:, 16 * h:16 * h + 16]), qk, ["qn%d" % h], 390)
        act(T.sn[:, lo:hi], T.st3[:, 0:512].indirect(T.posl[:, 16 * h:16 * h + 16]), qk, ["sn%d" % h], c=390)
    for h in range(2):
        lo, hi = 256 * h, 256 * h + 256
        b = mm(256, T.qv[:], T.sv[:], T.qn[:, lo:hi], T.sn[:, lo:hi], ["qv", "qn%d" % h, "sn%d" % h])
        store("y", T.oc[:, 4 * lo:4 * hi], T.qn[:, lo:hi].bitcast(dt.uint8), ["qn%d" % h])
        (cp if h else act)(T.ysb[:, lo:hi], T.ps[:, 512 * b:512 * b + 256], ["ps%d" % b, "sn1"], ["y%d" % h], c=212)
        store("y", T.y[:, lo:hi], T.ysb[:, lo:hi], ["y%d" % h])
    for k in range(4):
        store("s", T.osc[4 * k:4 * k + 4, :], T.sn[32 * k:32 * k + 4, :], ["sn0", "sn1", "y0"])

    for i in schedule(nodes, ready):
        nodes[i][4]()
    for s in sorted(count):
        g.wait_ge(T.sem[s], count[s])
